import numpy as np
import ml_dtypes


def mxq(x, axis, fmt="e4m3"):
    dtype, down = {"e4m3": (ml_dtypes.float8_e4m3fn, 7), "e5m2": (ml_dtypes.float8_e5m2, 14)}[fmt]
    v = np.moveaxis(np.asarray(x, np.float32).astype(ml_dtypes.bfloat16).astype(np.float64), axis, -1)
    blocks = v.reshape(v.shape[:-1] + (-1, 32))
    amax = np.abs(blocks).max(-1, keepdims=True)
    byte = np.maximum(np.where(amax > 0, np.frexp(amax)[1] - 1 + 127, 0) - down, 1)
    scale = np.exp2(byte - 127.0)
    codes = (blocks / scale).astype(np.float32).astype(dtype).astype(np.float64)
    return np.moveaxis((codes * scale).reshape(v.shape), -1, axis)


WIDE = False


def mx_kscale(k):
    if not WIDE:
        return np.ones(k)
    levels = np.array([10, -10, 5, -5, 0])
    if k % 512:
        return np.exp2(np.random.permutation(np.resize(levels, k // 32))).repeat(32)
    a = np.empty((k // 512, 16))
    for p in range(k // 512):
        a[p, :8] = np.random.permutation(np.resize(levels, 8))
        for g in range(8):
            far = levels[np.abs(levels - a[p, g]) >= 10]
            a[p, g + 8] = far[np.random.randint(len(far))]
    return np.exp2(a.ravel()).repeat(32)


def f64(x):
    return np.asarray(x).astype(np.float64)


def striped(idx):
    return np.tile(idx.reshape(-1, 16).T, (8, 1)).astype(np.uint16)


def unstriped(offs):
    return offs[:16].T.reshape(-1).astype(np.int64)


E2M1 = np.array([0.0, 0.5, 1.0, 1.5, 2.0, 3.0, 4.0, 6.0, -0.0, -0.5, -1.0, -1.5, -2.0, -3.0, -4.0, -6.0])


def pack_weight(w, fmt):
    k, n = w.shape
    w = f64(np.asarray(w, np.float32).astype(ml_dtypes.bfloat16)).reshape(k // 32, 32, n)
    amax = np.abs(w).max(1)
    if fmt == "e4m3":
        byte = np.frexp(amax)[1] - 1 + 127 - 7
    else:
        mant, ex = np.frexp(amax / 6.0)
        byte = np.where(mant > 0.5, ex, ex - 1) + 127
    byte = np.clip(np.where(amax > 0, byte, 1), 1, 254)
    scaled = (w * np.exp2(127.0 - byte)[:, None, :]).reshape(k, n).astype(np.float32)
    by_word = np.ascontiguousarray(scaled.reshape(k // 512, 128, 4, n).transpose(0, 1, 3, 2))
    if fmt == "e4m3":
        words = by_word.astype(ml_dtypes.float8_e4m3fn).view(np.uint8)
    else:
        c = by_word.astype(ml_dtypes.float4_e2m1fn).view(np.uint8) & 0xF
        words = (c[..., 0::2] | (c[..., 1::2] << 4)).reshape(k // 512, 128, 2 * n)
    return np.ascontiguousarray(words), np.ascontiguousarray(byte.astype(np.uint8).reshape(k // 512, 16, n))


def unpack_weight(words, scales, fmt):
    g, _, n = scales.shape
    words = np.ascontiguousarray(words).reshape(g, 128, n, -1)
    if fmt == "e4m3":
        vals = words.view(ml_dtypes.float8_e4m3fn).astype(np.float64)
    else:
        nib = np.empty((g, 128, n, 4), np.uint8)
        nib[..., 0::2] = words & 0xF
        nib[..., 1::2] = words >> 4
        vals = E2M1[nib]
    vals = vals * np.repeat(np.exp2(scales.astype(np.float64) - 127.0), 8, axis=1)[..., None]
    return vals.transpose(0, 1, 3, 2).reshape(g * 512, n)


def silu(v):
    return v / (1.0 + np.exp(-np.maximum(v, -700.0)))


K, T, S, H, N = 512, 1024, 512, 512, 512


def setup_inputs():
    n = np.random.standard_normal
    s = mx_kscale(K)
    u = mx_kscale(H)
    hard = np.random.permutation(T)[:S]
    x = pack_weight(n((K, T)) * s[:, None], "e4m3")
    w = pack_weight(n((K, N)) / np.sqrt(K) / s[:, None], "e2m1")
    w1 = pack_weight(n((K, H)) / np.sqrt(K) / s[:, None], "e4m3")
    w3 = pack_weight(n((K, H)) / np.sqrt(K) / s[:, None] * u, "e4m3")
    w2 = pack_weight(n((H, N)) / np.sqrt(H) / u[:, None], "e4m3")
    return {
        "x_words": x[0],
        "x_scales": x[1],
        "w_words": w[0],
        "w_scales": w[1],
        "w1_words": w1[0],
        "w1_scales": w1[1],
        "w3_words": w3[0],
        "w3_scales": w3[1],
        "w2_words": w2[0],
        "w2_scales": w2[1],
        "offs": striped(hard),
    }


def reference(x_words, x_scales, w_words, w_scales, w1_words, w1_scales, w3_words, w3_scales, w2_words, w2_scales, offs):
    w = unpack_weight(w_words, w_scales, "e2m1")
    w1 = unpack_weight(w1_words, w1_scales, "e4m3")
    w3 = unpack_weight(w3_words, w3_scales, "e4m3")
    w2 = unpack_weight(w2_words, w2_scales, "e4m3")
    idx = unstriped(offs)
    x = unpack_weight(x_words, x_scales, "e4m3")
    out = w.T @ x
    h = silu(w1.T @ x[:, idx]) * (w3.T @ x[:, idx])
    out[:, idx] = w2.T @ mxq(h, 0, "e4m3")
    return out

@@ -1,0 +1,194 @@
+from contextlib import ExitStack
+
+import concourse.mybir as mybir
+from concourse.masks import make_identity
+
+K, T, S, H, N = 512, 1024, 512, 512, 512
+FLOPS = 2 * K * N * T + 2 * S * (2 * K * H + H * N)
+
+F32 = mybir.dt.float32
+BF16 = mybir.dt.bfloat16
+I32 = mybir.dt.int32
+U32 = mybir.dt.uint32
+U16 = mybir.dt.uint16
+U8 = mybir.dt.uint8
+FP8X4 = mybir.dt.float8_e4m3fn_x4
+FP4X4 = mybir.dt.float4_e2m1fn_x4
+ACT = mybir.ActivationFunctionType
+MULT = mybir.AluOpType.mult
+
+P = 128
+BANK = 512
+CHUNKS = S // P
+ROW_BLOCKS = N // P
+LIST_ROWS = 16
+
+
+def tile_moe_cas_glu_silu_kernel(
+    tc, x_words, x_scales, w_words, w_scales, w1_words, w1_scales, w3_words, w3_scales, w2_words, w2_scales, offs, out
+):
+    nc = tc.nc
+    with ExitStack() as ctx:
+        keep = ctx.enter_context(tc.tile_pool(name="keep", bufs=1))
+        psum = ctx.enter_context(tc.psum_pool(name="psum", bufs=1))
+
+        def zeroed_plane(engine, name, width):
+            plane = keep.tile([P, width], U8, name=name, align_bytes=64)
+            engine.memset(plane[:].bitcast(I32), 0)
+            return plane
+
+        def load_plane(plane, scales, queues):
+            rows = scales[0].bitcast(I32).rearrange("(q r) n -> r q n", r=4)
+            for r in range(4):
+                queues[r].dma_start(out=plane[r:P:32, :].bitcast(I32), in_=rows[r])
+
+        def load_words(name, words, queue):
+            tile = keep.tile([P, words.shape[2]], I32, name=name, align_bytes=64)
+            queue.dma_start(out=tile[:], in_=words[0].rearrange("p n d -> p (n d)").bitcast(I32))
+            return tile
+
+        def bank_tile(shape, name, bank):
+            return psum.tile(shape, F32, name=name, offset=bank * 4 * BANK)
+
+        x_plane = zeroed_plane(nc.vector, "x_plane", T)[:]
+        w1_plane = zeroed_plane(nc.vector, "w1_plane", H)[:]
+        w3_plane = zeroed_plane(nc.vector, "w3_plane", H)[:]
+        w_plane = zeroed_plane(nc.vector, "w_plane", N)[:]
+        w2_plane = zeroed_plane(nc.vector, "w2_plane", N)[:]
+
+        offsets = keep.tile([P, S // LIST_ROWS], U16, name="offsets")
+        nc.sync.dma_start(offsets[:], offs)
+        x_sb = load_words("x_sb", x_words, nc.scalar)
+        w1_sb = load_words("w1_sb", w1_words, nc.gpsimd)
+        w3_sb = load_words("w3_sb", w3_words, nc.gpsimd)
+        w2_sb = load_words("w2_sb", w2_words, nc.gpsimd)
+        load_plane(x_plane, x_scales, [nc.sync, nc.scalar] * 2)
+        load_plane(w1_plane, w1_scales, [nc.sync, nc.scalar, nc.sync, nc.sync])
+        w_sb = keep.tile([P, 2 * N], U8, name="w_sb", align_bytes=64)
+        nc.scalar.dma_start(out=w_sb[:].bitcast(I32), in_=w_words[0].bitcast(I32))
+        load_plane(w3_plane, w3_scales, [nc.sync] * 4)
+        load_plane(w_plane, w_scales, [nc.sync] * 4)
+        load_plane(w2_plane, w2_scales, [nc.sync] * 4)
+
+        warm = keep.tile([P, 2], F32, name="warm")
+        nc.vector.memset(warm[:, 0:1], 0.0)
+        nc.scalar.activation(out=warm[:, 1:2], in_=warm[:, 0:1], func=ACT.Silu)
+        ident = keep.tile([P, P], F32, name="ident")
+        make_identity(nc, ident[:])
+
+        def listed(first, count):
+            return offsets[:, first // LIST_ROWS : (first + count) // LIST_ROWS]
+
+        slot_words, slot_planes = {}, {}
+
+        def gather(first_chunk, chunks):
+            width = chunks * P
+            words = keep.tile([P, width], U32, name="slot_words%d" % first_chunk, align_bytes=64)
+            plane = keep.tile([P, width], U8, name="slot_plane%d" % first_chunk, align_bytes=64)
+            entries = listed(first_chunk * P, width)
+            nc.vector.tensor_copy(words[:], x_sb[:].bitcast(U32).indirect(entries))
+            nc.vector.tensor_copy(plane[:], x_plane.indirect(entries))
+            for c in range(chunks):
+                slot_words[first_chunk + c] = words[:, c * P : (c + 1) * P]
+                slot_planes[first_chunk + c] = plane[:, c * P : (c + 1) * P]
+
+        hidden = {}
+
+        def first_layer(c):
+            by_pair = "j (p u e) -> j u p e"
+            as_pair = "j (u p e) -> j u p e"
+            sums = []
+            for bank_number, words, plane in ((c % 2, w1_sb, w1_plane), (2 + c, w3_sb, w3_plane)):
+                bank = bank_tile([P, BANK], "a%d_%d" % (bank_number, c), bank_number)
+                nc.tensor.matmul_mx(
+                    out=bank[:],
+                    lhsT=slot_words[c].bitcast(FP8X4),
+                    lhsT_scale=slot_planes[c],
+                    rhs=words[:].bitcast(FP8X4),
+                    rhs_scale=plane,
+                    start=True,
+                    stop=True,
+                )
+                sums.append(bank[:].rearrange(by_pair, u=2, e=2))
+            gate = keep.tile([P, H], F32, name="gate%d" % c)
+            nc.scalar.activation(out=gate[:].rearrange(as_pair, u=2, e=2), in_=sums[0], func=ACT.Silu)
+            hidden[c] = keep.tile([P, H], BF16, name="hidden%d" % c, align_bytes=64)
+            nc.vector.tensor_tensor(
+                hidden[c][:].rearrange(as_pair, u=2, e=2), sums[1], gate[:].rearrange(as_pair, u=2, e=2), MULT
+            )
+
+        z_sb = [keep.tile([P, S], F32, name="z_sb%d" % r) for r in range(ROW_BLOCKS)]
+        h_words = keep.tile([P, S], U32, name="h_words", align_bytes=64)
+        h_plane = keep.tile([P, S], U8, name="h_plane", align_bytes=64)
+
+        def quantise_hidden(c):
+            pairs = hidden[c][:].bitcast(F32)
+            turned = bank_tile([P, 2, P], "turned%d" % c, 2 + c)
+            for u in range(2):
+                nc.tensor.transpose(turned[:, u, :], pairs[:, u * P : (u + 1) * P], ident[:])
+            grouped = keep.tile([P, 4 * P], BF16, name="grouped%d" % c, align_bytes=64)
+            nc.scalar.copy(
+                out=grouped[:].bitcast(F32).rearrange("p (j u) -> p j u", u=2),
+                in_=turned[:].rearrange("p u j -> p j u"),
+            )
+            slots = slice(c * P, (c + 1) * P)
+            nc.vector.quantize_mx(out=h_words[:, slots].bitcast(FP8X4), scales=h_plane[:, slots], in_=grouped[:])
+
+        def second_layer(r, first, count, bank_number):
+            slots = slice(first, first + count)
+            cols = slice(r * P, (r + 1) * P)
+            bank = bank_tile([P, count], "z%d_%d" % (r, first), bank_number)
+            nc.tensor.matmul_mx(
+                out=bank[:],
+                lhsT=w2_sb[:, cols].bitcast(FP8X4),
+                lhsT_scale=w2_plane[:, cols],
+                rhs=h_words[:, slots].bitcast(FP8X4),
+                rhs_scale=h_plane[:, slots],
+                start=True,
+                stop=True,
+            )
+            nc.scalar.copy(out=z_sb[r][:, slots], in_=bank[:])
+
+        windows = {}
+
+        def light_layer(r, banks, copies):
+            windows[r] = keep.tile([P, T], F32, name="window%d" % r)
+            for half in range(T // BANK):
+                tokens = slice(half * BANK, (half + 1) * BANK)
+                bank = bank_tile([P, BANK], "y%d_%d" % (r, half), banks[half])
+                nc.tensor.matmul_mx(
+                    out=bank[:],
+                    lhsT=w_sb[:, 2 * r * P : 2 * (r + 1) * P].bitcast(FP4X4),
+                    lhsT_scale=w_plane[:, r * P : (r + 1) * P],
+                    rhs=x_sb[:, tokens].bitcast(FP8X4),
+                    rhs_scale=x_plane[:, tokens],
+                    start=True,
+                    stop=True,
+                )
+                copies[half](out=windows[r][:, tokens], in_=bank[:])
+
+        def scatter(r, first, count):
+            nc.vector.tensor_copy(windows[r][:].indirect(listed(first, count)), z_sb[r][:, first : first + count])
+
+        gather(0, 1)
+        gather(1, 1)
+        gather(2, 2)
+        for c in range(CHUNKS):
+            first_layer(c)
+        quantise_hidden(0)
+        second_layer(0, 0, P, 2)
+        quantise_hidden(1)
+        light_layer(0, (0, 1), (nc.scalar.copy, nc.vector.tensor_copy))
+        quantise_hidden(2)
+        quantise_hidden(3)
+        for c in range(1, CHUNKS):
+            second_layer(0, c * P, P, 2 + c)
+        scatter(0, 0, P)
+        scatter(0, P, P)
+        scatter(0, 2 * P, 2 * P)
+        nc.sync.dma_start(out=out[0:P, :], in_=windows[0][:])
+        for r in range(1, ROW_BLOCKS):
+            light_layer(r, (3, 4), (nc.scalar.copy, nc.scalar.copy))
+            second_layer(r, 0, S, 5)
+            scatter(r, 0, S)
+            nc.sync.dma_start(out=out[r * P : (r + 1) * P, :], in_=windows[r][:])

@@ -50,6 +50,8 @@ def tile_moe_cas_glu_silu_kernel(
         def bank_tile(shape, name, bank):
             return psum.tile(shape, F32, name=name, offset=bank * 4 * BANK)
 
+        warm = keep.tile([P, 2], F32, name="warm")
+        nc.vector.memset(warm[:, 0:1], 0.0)
         x_plane = zeroed_plane(nc.vector, "x_plane", T)[:]
         w1_plane = zeroed_plane(nc.vector, "w1_plane", H)[:]
         w3_plane = zeroed_plane(nc.vector, "w3_plane", H)[:]
@@ -61,20 +63,17 @@ def tile_moe_cas_glu_silu_kernel(
         x_sb = load_words("x_sb", x_words, nc.scalar)
         w1_sb = load_words("w1_sb", w1_words, nc.gpsimd)
         w3_sb = load_words("w3_sb", w3_words, nc.gpsimd)
-        w2_sb = load_words("w2_sb", w2_words, nc.gpsimd)
-        load_plane(x_plane, x_scales, [nc.sync, nc.scalar] * 2)
-        load_plane(w1_plane, w1_scales, [nc.sync, nc.scalar, nc.sync, nc.sync])
-        w_sb = keep.tile([P, 2 * N], U8, name="w_sb", align_bytes=64)
-        nc.scalar.dma_start(out=w_sb[:].bitcast(I32), in_=w_words[0].bitcast(I32))
-        load_plane(w3_plane, w3_scales, [nc.sync] * 4)
-        load_plane(w_plane, w_scales, [nc.sync] * 4)
-        load_plane(w2_plane, w2_scales, [nc.sync] * 4)
-
-        warm = keep.tile([P, 2], F32, name="warm")
-        nc.vector.memset(warm[:, 0:1], 0.0)
         nc.scalar.activation(out=warm[:, 1:2], in_=warm[:, 0:1], func=ACT.Silu)
         ident = keep.tile([P, P], F32, name="ident")
         make_identity(nc, ident[:])
+        load_plane(x_plane, x_scales, [nc.sync] * 4)
+        load_plane(w1_plane, w1_scales, [nc.scalar] * 4)
+        load_plane(w3_plane, w3_scales, [nc.sync] * 4)
+        w2_sb = load_words("w2_sb", w2_words, nc.sync)
+        w_sb = keep.tile([P, 2 * N], U8, name="w_sb", align_bytes=64)
+        nc.scalar.dma_start(out=w_sb[:].bitcast(I32), in_=w_words[0].bitcast(I32))
+        load_plane(w_plane, w_scales, [nc.scalar] * 4)
+        load_plane(w2_plane, w2_scales, [nc.scalar] * 4)
 
         def listed(first, count):
             return offsets[:, first // LIST_ROWS : (first + count) // LIST_ROWS]
@@ -98,7 +97,7 @@ def tile_moe_cas_glu_silu_kernel(
             by_pair = "j (p u e) -> j u p e"
             as_pair = "j (u p e) -> j u p e"
             sums = []
-            for bank_number, words, plane in ((c % 2, w1_sb, w1_plane), (2 + c, w3_sb, w3_plane)):
+            for bank_number, words, plane in ((c, w1_sb, w1_plane), (4 + c, w3_sb, w3_plane)):
                 bank = bank_tile([P, BANK], "a%d_%d" % (bank_number, c), bank_number)
                 nc.tensor.matmul_mx(
                     out=bank[:],
@@ -123,7 +122,7 @@ def tile_moe_cas_glu_silu_kernel(
 
         def quantise_hidden(c):
             pairs = hidden[c][:].bitcast(F32)
-            turned = bank_tile([P, 2, P], "turned%d" % c, 2 + c)
+            turned = bank_tile([P, 2, P], "turned%d" % c, 4 + c)
             for u in range(2):
                 nc.tensor.transpose(turned[:, u, :], pairs[:, u * P : (u + 1) * P], ident[:])
             grouped = keep.tile([P, 4 * P], BF16, name="grouped%d" % c, align_bytes=64)
@@ -170,25 +169,35 @@ def tile_moe_cas_glu_silu_kernel(
         def scatter(r, first, count):
             nc.vector.tensor_copy(windows[r][:].indirect(listed(first, count)), z_sb[r][:, first : first + count])
 
+        for half in range(2):
+            nc.tensor.matmul_mx(
+                out=bank_tile([P, BANK], "warm_pe%d" % half, 2 + half)[:],
+                lhsT=x_sb[:, 0:P].bitcast(FP8X4),
+                lhsT_scale=x_plane[:, 0:P],
+                rhs=x_sb[:, half * BANK : (half + 1) * BANK].bitcast(FP8X4),
+                rhs_scale=x_plane[:, half * BANK : (half + 1) * BANK],
+                start=True,
+                stop=True,
+            )
         gather(0, 1)
         gather(1, 1)
         gather(2, 2)
         for c in range(CHUNKS):
             first_layer(c)
         quantise_hidden(0)
-        second_layer(0, 0, P, 2)
+        second_layer(0, 0, P, 4)
         quantise_hidden(1)
-        light_layer(0, (0, 1), (nc.scalar.copy, nc.vector.tensor_copy))
+        light_layer(0, (2, 3), (nc.scalar.copy, nc.vector.tensor_copy))
         quantise_hidden(2)
         quantise_hidden(3)
         for c in range(1, CHUNKS):
-            second_layer(0, c * P, P, 2 + c)
+            second_layer(0, c * P, P, 4 + c)
         scatter(0, 0, P)
         scatter(0, P, P)
         scatter(0, 2 * P, 2 * P)
         nc.sync.dma_start(out=out[0:P, :], in_=windows[0][:])
         for r in range(1, ROW_BLOCKS):
-            light_layer(r, (3, 4), (nc.scalar.copy, nc.scalar.copy))
-            second_layer(r, 0, S, 5)
+            light_layer(r, (5, 6), (nc.scalar.copy, nc.scalar.copy))
+            second_layer(r, 0, S, 7)
             scatter(r, 0, S)
             nc.sync.dma_start(out=out[r * P : (r + 1) * P, :], in_=windows[r][:])

@@ -37,11 +37,6 @@ def tile_moe_cas_glu_silu_kernel(
             engine.memset(plane[:].bitcast(I32), 0)
             return plane
 
-        def load_plane(plane, scales, queues):
-            rows = scales[0].bitcast(I32).rearrange("(q r) n -> r q n", r=4)
-            for r in range(4):
-                queues[r].dma_start(out=plane[r:P:32, :].bitcast(I32), in_=rows[r])
-
         def load_words(name, words, queue):
             tile = keep.tile([P, words.shape[2]], I32, name=name, align_bytes=64)
             queue.dma_start(out=tile[:], in_=words[0].rearrange("p n d -> p (n d)").bitcast(I32))
@@ -50,87 +45,109 @@ def tile_moe_cas_glu_silu_kernel(
         def bank_tile(shape, name, bank):
             return psum.tile(shape, F32, name=name, offset=bank * 4 * BANK)
 
+        def bare_plane(name, width):
+            return keep.tile([P, width], U8, name=name, align_bytes=64)[:]
+
+        def load_rows(plane, scales, rows, queue):
+            by_row = scales[0].bitcast(I32).rearrange("(q r) n -> r q n", r=4)
+            for r in rows:
+                queue.dma_start(out=plane[r:P:32, :].bitcast(I32), in_=by_row[r])
+
+        def load_repeated(plane, scales, rows, queue):
+            by_quadrant = scales[0].bitcast(I32).rearrange("(q r) n -> q r n", r=4)
+            for q in rows:
+                source = by_quadrant[q].unsqueeze(0).to_broadcast([8, 4, by_quadrant.shape[2]])
+                queue.dma_start(out=plane[32 * q : 32 * (q + 1), :].bitcast(I32), in_=source)
+
+        x_plane = bare_plane("x_plane", T)
         warm = keep.tile([P, 2], F32, name="warm")
         nc.vector.memset(warm[:, 0:1], 0.0)
-        x_plane = zeroed_plane(nc.vector, "x_plane", T)[:]
-        w1_plane = zeroed_plane(nc.vector, "w1_plane", H)[:]
-        w3_plane = zeroed_plane(nc.vector, "w3_plane", H)[:]
-        w_plane = zeroed_plane(nc.vector, "w_plane", N)[:]
-        w2_plane = zeroed_plane(nc.vector, "w2_plane", N)[:]
+        w1_plane = bare_plane("w1_plane", H)
+        w3_plane = bare_plane("w3_plane", H)
+        w_plane = bare_plane("w_plane", N)
+        w2_plane = bare_plane("w2_plane", N)
 
+        w1_sb = load_words("w1_sb", w1_words, nc.sync)
         offsets = keep.tile([P, S // LIST_ROWS], U16, name="offsets")
         nc.sync.dma_start(offsets[:], offs)
+        load_repeated(x_plane, x_scales, (0, 1, 2), nc.scalar)
+        load_repeated(x_plane, x_scales, (3,), nc.sync)
+        load_rows(w1_plane, w1_scales, (0,), nc.sync)
         x_sb = load_words("x_sb", x_words, nc.scalar)
-        w1_sb = load_words("w1_sb", w1_words, nc.gpsimd)
-        w3_sb = load_words("w3_sb", w3_words, nc.gpsimd)
         nc.scalar.activation(out=warm[:, 1:2], in_=warm[:, 0:1], func=ACT.Silu)
+        load_rows(w3_plane, w3_scales, (0, 1), nc.gpsimd)
         ident = keep.tile([P, P], F32, name="ident")
         make_identity(nc, ident[:])
-        load_plane(x_plane, x_scales, [nc.sync] * 4)
-        load_plane(w1_plane, w1_scales, [nc.scalar] * 4)
-        load_plane(w3_plane, w3_scales, [nc.sync] * 4)
+        load_rows(w1_plane, w1_scales, (1, 2), nc.sync)
+        load_rows(w3_plane, w3_scales, (2, 3), nc.sync)
+        w3_sb = load_words("w3_sb", w3_words, nc.sync)
+        load_rows(w1_plane, w1_scales, (3,), nc.scalar)
+        load_rows(w_plane, w_scales, (0,), nc.sync)
+        w_first = keep.tile([P, 2 * P], U8, name="w_first", align_bytes=64)
+        nc.scalar.dma_start(out=w_first[:].bitcast(I32), in_=w_words[0][:, 0 : 2 * P].bitcast(I32))
+        load_rows(w_plane, w_scales, (1, 2), nc.sync)
         w2_sb = load_words("w2_sb", w2_words, nc.sync)
-        w_sb = keep.tile([P, 2 * N], U8, name="w_sb", align_bytes=64)
-        nc.scalar.dma_start(out=w_sb[:].bitcast(I32), in_=w_words[0].bitcast(I32))
-        load_plane(w_plane, w_scales, [nc.scalar] * 4)
-        load_plane(w2_plane, w2_scales, [nc.scalar] * 4)
+        load_rows(w2_plane, w2_scales, (0,), nc.sync)
+        load_rows(w_plane, w_scales, (3,), nc.sync)
+        load_rows(w2_plane, w2_scales, (1, 2, 3), nc.sync)
+        w_rest = keep.tile([P, 2 * (N - P)], U8, name="w_rest", align_bytes=64)
+        nc.sync.dma_start(out=w_rest[:].bitcast(I32), in_=w_words[0][:, 2 * P :].bitcast(I32))
+        w_blocks = [w_first[:]] + [w_rest[:, 2 * r * P : 2 * (r + 1) * P] for r in range(ROW_BLOCKS - 1)]
 
         def listed(first, count):
             return offsets[:, first // LIST_ROWS : (first + count) // LIST_ROWS]
 
-        slot_words, slot_planes = {}, {}
+        slot_plane = keep.tile([P, S], U8, name="slot_plane", align_bytes=64)
+        slot_words = {}
 
-        def gather(first_chunk, chunks):
-            width = chunks * P
-            words = keep.tile([P, width], U32, name="slot_words%d" % first_chunk, align_bytes=64)
-            plane = keep.tile([P, width], U8, name="slot_plane%d" % first_chunk, align_bytes=64)
-            entries = listed(first_chunk * P, width)
-            nc.vector.tensor_copy(words[:], x_sb[:].bitcast(U32).indirect(entries))
-            nc.vector.tensor_copy(plane[:], x_plane.indirect(entries))
-            for c in range(chunks):
-                slot_words[first_chunk + c] = words[:, c * P : (c + 1) * P]
-                slot_planes[first_chunk + c] = plane[:, c * P : (c + 1) * P]
+        def gather_words(c):
+            slot_words[c] = keep.tile([P, P], U32, name="slot_words%d" % c, align_bytes=64)
+            nc.vector.tensor_copy(slot_words[c][:], x_sb[:].bitcast(U32).indirect(listed(c * P, P)))
 
-        hidden = {}
+        def first_pass(c, bank_number, words, plane):
+            bank = bank_tile([P, BANK], "a%d_%d" % (c, bank_number), bank_number)
+            nc.tensor.matmul_mx(
+                out=bank[:],
+                lhsT=slot_words[c][:].bitcast(FP8X4),
+                lhsT_scale=slot_plane[:, c * P : (c + 1) * P],
+                rhs=words[:].bitcast(FP8X4),
+                rhs_scale=plane,
+                start=True,
+                stop=True,
+            )
+            return bank[:].rearrange("j (p u e) -> j u p e", u=2, e=2)
 
-        def first_layer(c):
-            by_pair = "j (p u e) -> j u p e"
-            as_pair = "j (u p e) -> j u p e"
-            sums = []
-            for bank_number, words, plane in ((c, w1_sb, w1_plane), (4 + c, w3_sb, w3_plane)):
-                bank = bank_tile([P, BANK], "a%d_%d" % (bank_number, c), bank_number)
-                nc.tensor.matmul_mx(
-                    out=bank[:],
-                    lhsT=slot_words[c].bitcast(FP8X4),
-                    lhsT_scale=slot_planes[c],
-                    rhs=words[:].bitcast(FP8X4),
-                    rhs_scale=plane,
-                    start=True,
-                    stop=True,
-                )
-                sums.append(bank[:].rearrange(by_pair, u=2, e=2))
-            gate = keep.tile([P, H], F32, name="gate%d" % c)
-            nc.scalar.activation(out=gate[:].rearrange(as_pair, u=2, e=2), in_=sums[0], func=ACT.Silu)
+        as_pair = "j (u p e) -> j u p e"
+        gates, hidden = {}, {}
+
+        def gate_half(c):
+            sums = first_pass(c, c, w1_sb, w1_plane)
+            gates[c] = keep.tile([P, H], F32, name="gate%d" % c)
+            nc.scalar.activation(out=gates[c][:].rearrange(as_pair, u=2, e=2), in_=sums, func=ACT.Silu)
+
+        def product_half(c):
+            sums = first_pass(c, CHUNKS + c, w3_sb, w3_plane)
             hidden[c] = keep.tile([P, H], BF16, name="hidden%d" % c, align_bytes=64)
             nc.vector.tensor_tensor(
-                hidden[c][:].rearrange(as_pair, u=2, e=2), sums[1], gate[:].rearrange(as_pair, u=2, e=2), MULT
+                hidden[c][:].rearrange(as_pair, u=2, e=2), sums, gates[c][:].rearrange(as_pair, u=2, e=2), MULT
             )
 
         z_sb = [keep.tile([P, S], F32, name="z_sb%d" % r) for r in range(ROW_BLOCKS)]
         h_words = keep.tile([P, S], U32, name="h_words", align_bytes=64)
         h_plane = keep.tile([P, S], U8, name="h_plane", align_bytes=64)
 
-        def quantise_hidden(c):
-            pairs = hidden[c][:].bitcast(F32)
-            turned = bank_tile([P, 2, P], "turned%d" % c, 4 + c)
-            for u in range(2):
-                nc.tensor.transpose(turned[:, u, :], pairs[:, u * P : (u + 1) * P], ident[:])
-            grouped = keep.tile([P, 4 * P], BF16, name="grouped%d" % c, align_bytes=64)
+        def quantise_hidden(first_chunk, chunks, bank_number):
+            turned = bank_tile([P, chunks, 2, P], "turned%d" % first_chunk, bank_number)
+            for c in range(chunks):
+                pairs = hidden[first_chunk + c][:].bitcast(F32)
+                for u in range(2):
+                    nc.tensor.transpose(turned[:, c, u, :], pairs[:, u * P : (u + 1) * P], ident[:])
+            grouped = keep.tile([P, chunks * 4 * P], BF16, name="grouped%d" % first_chunk, align_bytes=64)
             nc.scalar.copy(
-                out=grouped[:].bitcast(F32).rearrange("p (j u) -> p j u", u=2),
-                in_=turned[:].rearrange("p u j -> p j u"),
+                out=grouped[:].bitcast(F32).rearrange("p (c j u) -> p c j u", c=chunks, u=2),
+                in_=turned[:].rearrange("p c u j -> p c j u"),
             )
-            slots = slice(c * P, (c + 1) * P)
+            slots = slice(first_chunk * P, (first_chunk + chunks) * P)
             nc.vector.quantize_mx(out=h_words[:, slots].bitcast(FP8X4), scales=h_plane[:, slots], in_=grouped[:])
 
         def second_layer(r, first, count, bank_number):
@@ -157,7 +174,7 @@ def tile_moe_cas_glu_silu_kernel(
                 bank = bank_tile([P, BANK], "y%d_%d" % (r, half), banks[half])
                 nc.tensor.matmul_mx(
                     out=bank[:],
-                    lhsT=w_sb[:, 2 * r * P : 2 * (r + 1) * P].bitcast(FP4X4),
+                    lhsT=w_blocks[r].bitcast(FP4X4),
                     lhsT_scale=w_plane[:, r * P : (r + 1) * P],
                     rhs=x_sb[:, tokens].bitcast(FP8X4),
                     rhs_scale=x_plane[:, tokens],
@@ -172,32 +189,44 @@ def tile_moe_cas_glu_silu_kernel(
         for half in range(2):
             nc.tensor.matmul_mx(
                 out=bank_tile([P, BANK], "warm_pe%d" % half, 2 + half)[:],
-                lhsT=x_sb[:, 0:P].bitcast(FP8X4),
+                lhsT=w1_sb[:, 0:P].bitcast(FP8X4),
                 lhsT_scale=x_plane[:, 0:P],
-                rhs=x_sb[:, half * BANK : (half + 1) * BANK].bitcast(FP8X4),
+                rhs=w1_sb[:].bitcast(FP8X4),
                 rhs_scale=x_plane[:, half * BANK : (half + 1) * BANK],
                 start=True,
                 stop=True,
             )
-        gather(0, 1)
-        gather(1, 1)
-        gather(2, 2)
+        nc.vector.tensor_copy(slot_plane[:], x_plane.indirect(offsets[:]))
         for c in range(CHUNKS):
-            first_layer(c)
-        quantise_hidden(0)
-        second_layer(0, 0, P, 4)
-        quantise_hidden(1)
-        light_layer(0, (2, 3), (nc.scalar.copy, nc.vector.tensor_copy))
-        quantise_hidden(2)
-        quantise_hidden(3)
-        for c in range(1, CHUNKS):
-            second_layer(0, c * P, P, 4 + c)
-        scatter(0, 0, P)
-        scatter(0, P, P)
-        scatter(0, 2 * P, 2 * P)
-        nc.sync.dma_start(out=out[0:P, :], in_=windows[0][:])
-        for r in range(1, ROW_BLOCKS):
-            light_layer(r, (5, 6), (nc.scalar.copy, nc.scalar.copy))
-            second_layer(r, 0, S, 7)
-            scatter(r, 0, S)
+            gather_words(c)
+        gate_half(0)
+        for c in range(CHUNKS):
+            if c + 1 < CHUNKS:
+                gate_half(c + 1)
+            product_half(c)
+        both_scalar = (nc.scalar.copy, nc.scalar.copy)
+        half = S // 2
+
+        def store(r):
             nc.sync.dma_start(out=out[r * P : (r + 1) * P, :], in_=windows[r][:])
+
+        quantise_hidden(0, 1, 4)
+        quantise_hidden(1, 1, 5)
+        light_layer(0, (0, 1), (nc.scalar.copy, nc.vector.tensor_copy))
+        second_layer(0, 0, half, 4)
+        scatter(0, 0, half)
+        second_layer(1, 0, half, 5)
+        light_layer(1, (2, 3), both_scalar)
+        scatter(1, 0, half)
+        quantise_hidden(2, 2, 4)
+        light_layer(2, (2, 3), both_scalar)
+        second_layer(2, 0, half, 5)
+        scatter(2, 0, half)
+        for r in range(3):
+            second_layer(r, half, half, (0, 1, 5)[r])
+            scatter(r, half, half)
+            store(r)
+        light_layer(3, (2, 3), both_scalar)
+        second_layer(3, 0, S, 6)
+        scatter(3, 0, S)
+        store(3)

@@ -48,10 +48,13 @@ def tile_moe_cas_glu_silu_kernel(
         def bare_plane(name, width):
             return keep.tile([P, width], U8, name=name, align_bytes=64)[:]
 
-        def load_rows(plane, scales, rows, queue):
-            by_row = scales[0].bitcast(I32).rearrange("(q r) n -> r q n", r=4)
-            for r in rows:
-                queue.dma_start(out=plane[r:P:32, :].bitcast(I32), in_=by_row[r])
+        def load_upper(plane, scales, queue):
+            rows = scales[0].bitcast(I32)[2:16, :]
+            source = rows.unsqueeze(0).to_broadcast([5, 14, rows.shape[1]])
+            queue.dma_start(out=plane[30:100, :].bitcast(I32), in_=source)
+
+        def load_lower(plane, scales, queue):
+            queue.dma_start(out=plane[0:4, :].bitcast(I32), in_=scales[0].bitcast(I32)[0:4, :])
 
         def load_repeated(plane, scales, rows, queue):
             by_quadrant = scales[0].bitcast(I32).rearrange("(q r) n -> q r n", r=4)
@@ -72,27 +75,23 @@ def tile_moe_cas_glu_silu_kernel(
         nc.sync.dma_start(offsets[:], offs)
         load_repeated(x_plane, x_scales, (0, 1, 2), nc.scalar)
         load_repeated(x_plane, x_scales, (3,), nc.sync)
-        load_rows(w1_plane, w1_scales, (0,), nc.sync)
+        load_upper(w1_plane, w1_scales, nc.sync)
         x_sb = load_words("x_sb", x_words, nc.scalar)
-        nc.scalar.activation(out=warm[:, 1:2], in_=warm[:, 0:1], func=ACT.Silu)
-        load_rows(w3_plane, w3_scales, (0, 1), nc.gpsimd)
+        load_lower(w1_plane, w1_scales, nc.sync)
+        load_lower(w3_plane, w3_scales, nc.gpsimd)
         ident = keep.tile([P, P], F32, name="ident")
         make_identity(nc, ident[:])
-        load_rows(w1_plane, w1_scales, (1, 2), nc.sync)
-        load_rows(w3_plane, w3_scales, (2, 3), nc.sync)
-        w3_sb = load_words("w3_sb", w3_words, nc.sync)
-        load_rows(w1_plane, w1_scales, (3,), nc.scalar)
-        load_rows(w_plane, w_scales, (0,), nc.sync)
-        w_first = keep.tile([P, 2 * P], U8, name="w_first", align_bytes=64)
-        nc.scalar.dma_start(out=w_first[:].bitcast(I32), in_=w_words[0][:, 0 : 2 * P].bitcast(I32))
-        load_rows(w_plane, w_scales, (1, 2), nc.sync)
+        load_upper(w3_plane, w3_scales, nc.sync)
+        w3_sb = load_words("w3_sb", w3_words, nc.scalar)
+        nc.scalar.activation(out=warm[:, 1:2], in_=warm[:, 0:1], func=ACT.Silu)
+        load_upper(w_plane, w_scales, nc.sync)
+        w_sb = keep.tile([P, 2 * N], U8, name="w_sb", align_bytes=64)
+        nc.sync.dma_start(out=w_sb[:].bitcast(I32), in_=w_words[0].bitcast(I32))
+        load_upper(w2_plane, w2_scales, nc.sync)
         w2_sb = load_words("w2_sb", w2_words, nc.sync)
-        load_rows(w2_plane, w2_scales, (0,), nc.sync)
-        load_rows(w_plane, w_scales, (3,), nc.sync)
-        load_rows(w2_plane, w2_scales, (1, 2, 3), nc.sync)
-        w_rest = keep.tile([P, 2 * (N - P)], U8, name="w_rest", align_bytes=64)
-        nc.sync.dma_start(out=w_rest[:].bitcast(I32), in_=w_words[0][:, 2 * P :].bitcast(I32))
-        w_blocks = [w_first[:]] + [w_rest[:, 2 * r * P : 2 * (r + 1) * P] for r in range(ROW_BLOCKS - 1)]
+        load_lower(w_plane, w_scales, nc.sync)
+        load_lower(w2_plane, w2_scales, nc.sync)
+        w_blocks = [w_sb[:, 2 * r * P : 2 * (r + 1) * P] for r in range(ROW_BLOCKS)]
 
         def listed(first, count):
             return offsets[:, first // LIST_ROWS : (first + count) // LIST_ROWS]
@@ -212,21 +211,21 @@ def tile_moe_cas_glu_silu_kernel(
 
         quantise_hidden(0, 1, 4)
         quantise_hidden(1, 1, 5)
-        light_layer(0, (0, 1), (nc.scalar.copy, nc.vector.tensor_copy))
-        second_layer(0, 0, half, 4)
+        light_layer(0, (4, 5), (nc.scalar.copy, nc.vector.tensor_copy))
+        second_layer(0, 0, half, 0)
         scatter(0, 0, half)
-        second_layer(1, 0, half, 5)
-        light_layer(1, (2, 3), both_scalar)
+        second_layer(1, 0, half, 1)
+        light_layer(1, (4, 0), both_scalar)
         scatter(1, 0, half)
-        quantise_hidden(2, 2, 4)
-        light_layer(2, (2, 3), both_scalar)
-        second_layer(2, 0, half, 5)
+        quantise_hidden(2, 2, 1)
+        light_layer(2, (4, 0), both_scalar)
+        second_layer(2, 0, half, 1)
         scatter(2, 0, half)
         for r in range(3):
-            second_layer(r, half, half, (0, 1, 5)[r])
+            second_layer(r, half, half, (5, 2, 3)[r])
             scatter(r, half, half)
             store(r)
-        light_layer(3, (2, 3), both_scalar)
+        light_layer(3, (4, 0), both_scalar)
         second_layer(3, 0, S, 6)
         scatter(3, 0, S)
         store(3)

@@ -131,6 +131,7 @@ def tile_moe_cas_glu_silu_kernel(
                 hidden[c][:].rearrange(as_pair, u=2, e=2), sums, gates[c][:].rearrange(as_pair, u=2, e=2), MULT
             )
 
+        copy_of = (nc.vector.tensor_copy, nc.scalar.copy) * 2
         z_sb = [keep.tile([P, S], F32, name="z_sb%d" % r) for r in range(ROW_BLOCKS)]
         h_words = keep.tile([P, S], U32, name="h_words", align_bytes=64)
         h_plane = keep.tile([P, S], U8, name="h_plane", align_bytes=64)
@@ -162,11 +163,11 @@ def tile_moe_cas_glu_silu_kernel(
                 start=True,
                 stop=True,
             )
-            nc.scalar.copy(out=z_sb[r][:, slots], in_=bank[:])
+            copy_of[r](out=z_sb[r][:, slots], in_=bank[:])
 
         windows = {}
 
-        def light_layer(r, banks, copies):
+        def light_layer(r, banks):
             windows[r] = keep.tile([P, T], F32, name="window%d" % r)
             for half in range(T // BANK):
                 tokens = slice(half * BANK, (half + 1) * BANK)
@@ -180,10 +181,14 @@ def tile_moe_cas_glu_silu_kernel(
                     start=True,
                     stop=True,
                 )
-                copies[half](out=windows[r][:, tokens], in_=bank[:])
+                copy_of[r](out=windows[r][:, tokens], in_=bank[:])
 
         def scatter(r, first, count):
-            nc.vector.tensor_copy(windows[r][:].indirect(listed(first, count)), z_sb[r][:, first : first + count])
+            target = windows[r][:].indirect(listed(first, count))
+            if r % 2 == 0:
+                nc.vector.tensor_copy(target, z_sb[r][:, first : first + count])
+            else:
+                nc.scalar.activation(target, z_sb[r][:, first : first + count], ACT.Copy)
 
         for half in range(2):
             nc.tensor.matmul_mx(
@@ -203,7 +208,6 @@ def tile_moe_cas_glu_silu_kernel(
             if c + 1 < CHUNKS:
                 gate_half(c + 1)
             product_half(c)
-        both_scalar = (nc.scalar.copy, nc.scalar.copy)
         half = S // 2
 
         def store(r):
@@ -211,21 +215,21 @@ def tile_moe_cas_glu_silu_kernel(
 
         quantise_hidden(0, 1, 4)
         quantise_hidden(1, 1, 5)
-        light_layer(0, (4, 5), (nc.scalar.copy, nc.vector.tensor_copy))
-        second_layer(0, 0, half, 0)
-        scatter(0, 0, half)
-        second_layer(1, 0, half, 1)
-        light_layer(1, (4, 0), both_scalar)
-        scatter(1, 0, half)
-        quantise_hidden(2, 2, 1)
-        light_layer(2, (4, 0), both_scalar)
-        second_layer(2, 0, half, 1)
-        scatter(2, 0, half)
-        for r in range(3):
-            second_layer(r, half, half, (5, 2, 3)[r])
-            scatter(r, half, half)
-            store(r)
-        light_layer(3, (4, 0), both_scalar)
-        second_layer(3, 0, S, 6)
-        scatter(3, 0, S)
+        quantise_hidden(2, 2, 7)
+        light_layer(0, (0, 1))
+        light_layer(1, (2, 3))
+        for piece in range(2):
+            for r in range(2):
+                second_layer(r, piece * half, half, 4 + r + 2 * piece)
+                scatter(r, piece * half, half)
+        store(0)
+        store(1)
+        light_layer(2, (0, 1))
+        light_layer(3, (2, 3))
+        second_layer(2, 0, S, 4)
+        second_layer(3, 0, S, 5)
+        scatter(2, 0, S)
+        store(2)
+        scatter(3, 0, half)
+        scatter(3, half, half)
         store(3)

@@ -1,7 +1,6 @@
 from contextlib import ExitStack
 
 import concourse.mybir as mybir
-from concourse.masks import make_identity
 
 K, T, S, H, N = 512, 1024, 512, 512, 512
 FLOPS = 2 * K * N * T + 2 * S * (2 * K * H + H * N)
@@ -38,7 +37,7 @@ def tile_moe_cas_glu_silu_kernel(
             return plane
 
         def load_words(name, words, queue):
-            tile = keep.tile([P, words.shape[2]], I32, name=name, align_bytes=64)
+            tile = keep.tile([P, words.shape[2]], I32, name=name, tag=name, align_bytes=64)
             queue.dma_start(out=tile[:], in_=words[0].rearrange("p n d -> p (n d)").bitcast(I32))
             return tile
 
@@ -56,6 +55,14 @@ def tile_moe_cas_glu_silu_kernel(
         def load_lower(plane, scales, queue):
             queue.dma_start(out=plane[0:4, :].bitcast(I32), in_=scales[0].bitcast(I32)[0:4, :])
 
+        def load_upper_full(plane, scales, queue):
+            rows = scales[0].bitcast(I32)[2:16, :]
+            source = rows.unsqueeze(0).to_broadcast([8, 14, rows.shape[1]])
+            queue.dma_start(out=plane[16:128, :].bitcast(I32), in_=source)
+
+        def load_lower_full(plane, scales, queue):
+            queue.dma_start(out=plane[0:16, :].bitcast(I32), in_=scales[0].bitcast(I32))
+
         def load_repeated(plane, scales, rows, queue):
             by_quadrant = scales[0].bitcast(I32).rearrange("(q r) n -> q r n", r=4)
             for q in rows:
@@ -69,27 +76,25 @@ def tile_moe_cas_glu_silu_kernel(
         w3_plane = bare_plane("w3_plane", H)
         w_plane = bare_plane("w_plane", N)
         w2_plane = bare_plane("w2_plane", N)
-
-        w1_sb = load_words("w1_sb", w1_words, nc.sync)
         offsets = keep.tile([P, S // LIST_ROWS], U16, name="offsets")
-        nc.sync.dma_start(offsets[:], offs)
-        load_repeated(x_plane, x_scales, (0, 1, 2), nc.scalar)
-        load_repeated(x_plane, x_scales, (3,), nc.sync)
-        load_upper(w1_plane, w1_scales, nc.sync)
-        x_sb = load_words("x_sb", x_words, nc.scalar)
-        load_lower(w1_plane, w1_scales, nc.sync)
-        load_lower(w3_plane, w3_scales, nc.gpsimd)
-        ident = keep.tile([P, P], F32, name="ident")
-        make_identity(nc, ident[:])
-        load_upper(w3_plane, w3_scales, nc.sync)
-        w3_sb = load_words("w3_sb", w3_words, nc.scalar)
-        nc.scalar.activation(out=warm[:, 1:2], in_=warm[:, 0:1], func=ACT.Silu)
-        load_upper(w_plane, w_scales, nc.sync)
         w_sb = keep.tile([P, 2 * N], U8, name="w_sb", align_bytes=64)
+
+        nc.sync.dma_start(offsets[:], offs)
+        load_repeated(x_plane, x_scales, (0, 1), nc.scalar)
+        load_repeated(x_plane, x_scales, (2, 3), nc.sync)
+        w1_sb = load_words("w1_sb", w1_words, nc.scalar)
+        x_sb = load_words("x_sb", x_words, nc.sync)
+        load_upper_full(w1_plane, w1_scales, nc.scalar)
+        load_lower(w_plane, w_scales, nc.gpsimd)
+        load_lower_full(w1_plane, w1_scales, nc.scalar)
+        load_upper_full(w3_plane, w3_scales, nc.scalar)
+        nc.scalar.activation(out=warm[:, 1:2], in_=warm[:, 0:1], func=ACT.Silu)
+        load_lower_full(w3_plane, w3_scales, nc.sync)
+        w3_sb = load_words("w3_sb", w3_words, nc.sync)
         nc.sync.dma_start(out=w_sb[:].bitcast(I32), in_=w_words[0].bitcast(I32))
+        load_upper(w_plane, w_scales, nc.sync)
         load_upper(w2_plane, w2_scales, nc.sync)
         w2_sb = load_words("w2_sb", w2_words, nc.sync)
-        load_lower(w_plane, w_scales, nc.sync)
         load_lower(w2_plane, w2_scales, nc.sync)
         w_blocks = [w_sb[:, 2 * r * P : 2 * (r + 1) * P] for r in range(ROW_BLOCKS)]
 
@@ -99,36 +104,58 @@ def tile_moe_cas_glu_silu_kernel(
         slot_plane = keep.tile([P, S], U8, name="slot_plane", align_bytes=64)
         slot_words = {}
 
-        def gather_words(c):
-            slot_words[c] = keep.tile([P, P], U32, name="slot_words%d" % c, align_bytes=64)
-            nc.vector.tensor_copy(slot_words[c][:], x_sb[:].bitcast(U32).indirect(listed(c * P, P)))
+        def gather_words(first_chunk, chunks, tag):
+            tile = keep.tile([P, chunks * P], U32, name="slot_words%d" % first_chunk, tag=tag, align_bytes=64)
+            nc.vector.tensor_copy(tile[:], x_sb[:].bitcast(U32).indirect(listed(first_chunk * P, chunks * P)))
+            for c in range(chunks):
+                slot_words[first_chunk + c] = tile[:, c * P : (c + 1) * P]
+
+        def deal_words(name, words):
+            dealt = keep.tile([P, H], U32, name=name, align_bytes=64)
+            nc.scalar.copy(
+                out=dealt[:].rearrange("p (t g m) -> p g t m", t=4, m=4),
+                in_=words[:].bitcast(U32).rearrange("p (g m t) -> p g t m", m=4, t=4),
+            )
+            return dealt
+
+        def deal_scales(name, plane):
+            dealt = keep.tile([P, H], U8, name=name, align_bytes=64)
+            nc.vector.tensor_copy(
+                dealt[:].rearrange("p (t g m) -> p g t m", t=4, m=16),
+                plane.rearrange("p (g m t) -> p g t m", m=16, t=4),
+            )
+            return dealt
 
         def first_pass(c, bank_number, words, plane):
             bank = bank_tile([P, BANK], "a%d_%d" % (c, bank_number), bank_number)
-            nc.tensor.matmul_mx(
-                out=bank[:],
-                lhsT=slot_words[c][:].bitcast(FP8X4),
-                lhsT_scale=slot_plane[:, c * P : (c + 1) * P],
-                rhs=words[:].bitcast(FP8X4),
-                rhs_scale=plane,
-                start=True,
-                stop=True,
-            )
-            return bank[:].rearrange("j (p u e) -> j u p e", u=2, e=2)
+            for t in range(4):
+                cols = slice(t * P, (t + 1) * P)
+                nc.tensor.matmul_mx(
+                    out=bank[:, cols],
+                    lhsT=words[:, cols].bitcast(FP8X4),
+                    lhsT_scale=plane[:, cols],
+                    rhs=slot_words[c].bitcast(FP8X4),
+                    rhs_scale=slot_plane[:, c * P : (c + 1) * P],
+                    start=True,
+                    stop=True,
+                )
+            return bank[:].rearrange("p (t j) -> p j t", t=4)
 
-        as_pair = "j (u p e) -> j u p e"
-        gates, hidden = {}, {}
+        gates = {}
+        hidden = keep.tile([P, 4 * S], BF16, name="hidden", align_bytes=64)
 
-        def gate_half(c):
-            sums = first_pass(c, c, w1_sb, w1_plane)
+        def gate_half(c, bank_number):
+            sums = first_pass(c, bank_number, w1_dealt, w1_dealt_plane)
             gates[c] = keep.tile([P, H], F32, name="gate%d" % c)
-            nc.scalar.activation(out=gates[c][:].rearrange(as_pair, u=2, e=2), in_=sums, func=ACT.Silu)
+            nc.scalar.activation(out=gates[c][:].rearrange("p (j t) -> p j t", t=4), in_=sums, func=ACT.Silu)
 
-        def product_half(c):
-            sums = first_pass(c, CHUNKS + c, w3_sb, w3_plane)
-            hidden[c] = keep.tile([P, H], BF16, name="hidden%d" % c, align_bytes=64)
+        def product_half(c, bank_number):
+            sums = first_pass(c, bank_number, w3_dealt, w3_dealt_plane)
             nc.vector.tensor_tensor(
-                hidden[c][:].rearrange(as_pair, u=2, e=2), sums, gates[c][:].rearrange(as_pair, u=2, e=2), MULT
+                hidden[:, c * H : (c + 1) * H].rearrange("p (j t) -> p j t", t=4),
+                sums,
+                gates[c][:].rearrange("p (j t) -> p j t", t=4),
+                MULT,
             )
 
         copy_of = (nc.vector.tensor_copy, nc.scalar.copy) * 2
@@ -136,52 +163,48 @@ def tile_moe_cas_glu_silu_kernel(
         h_words = keep.tile([P, S], U32, name="h_words", align_bytes=64)
         h_plane = keep.tile([P, S], U8, name="h_plane", align_bytes=64)
 
-        def quantise_hidden(first_chunk, chunks, bank_number):
-            turned = bank_tile([P, chunks, 2, P], "turned%d" % first_chunk, bank_number)
-            for c in range(chunks):
-                pairs = hidden[first_chunk + c][:].bitcast(F32)
-                for u in range(2):
-                    nc.tensor.transpose(turned[:, c, u, :], pairs[:, u * P : (u + 1) * P], ident[:])
-            grouped = keep.tile([P, chunks * 4 * P], BF16, name="grouped%d" % first_chunk, align_bytes=64)
-            nc.scalar.copy(
-                out=grouped[:].bitcast(F32).rearrange("p (c j u) -> p c j u", c=chunks, u=2),
-                in_=turned[:].rearrange("p c u j -> p c j u"),
-            )
+        def quantise_hidden(first_chunk, chunks):
             slots = slice(first_chunk * P, (first_chunk + chunks) * P)
-            nc.vector.quantize_mx(out=h_words[:, slots].bitcast(FP8X4), scales=h_plane[:, slots], in_=grouped[:])
+            nc.vector.quantize_mx(
+                out=h_words[:, slots].bitcast(FP8X4),
+                scales=h_plane[:, slots],
+                in_=hidden[:, first_chunk * H : (first_chunk + chunks) * H],
+            )
 
-        def second_layer(r, first, count, bank_number):
-            slots = slice(first, first + count)
+        def second_layer(r, first, widths, bank_number):
+            count = sum(widths)
             cols = slice(r * P, (r + 1) * P)
             bank = bank_tile([P, count], "z%d_%d" % (r, first), bank_number)
-            nc.tensor.matmul_mx(
-                out=bank[:],
-                lhsT=w2_sb[:, cols].bitcast(FP8X4),
-                lhsT_scale=w2_plane[:, cols],
-                rhs=h_words[:, slots].bitcast(FP8X4),
-                rhs_scale=h_plane[:, slots],
-                start=True,
-                stop=True,
-            )
-            copy_of[r](out=z_sb[r][:, slots], in_=bank[:])
-
-        windows = {}
-
-        def light_layer(r, banks):
-            windows[r] = keep.tile([P, T], F32, name="window%d" % r)
-            for half in range(T // BANK):
-                tokens = slice(half * BANK, (half + 1) * BANK)
-                bank = bank_tile([P, BANK], "y%d_%d" % (r, half), banks[half])
+            done = 0
+            for width in widths:
+                slots = slice(first + done, first + done + width)
                 nc.tensor.matmul_mx(
-                    out=bank[:],
-                    lhsT=w_blocks[r].bitcast(FP4X4),
-                    lhsT_scale=w_plane[:, r * P : (r + 1) * P],
-                    rhs=x_sb[:, tokens].bitcast(FP8X4),
-                    rhs_scale=x_plane[:, tokens],
+                    out=bank[:, done : done + width],
+                    lhsT=w2_sb[:, cols].bitcast(FP8X4),
+                    lhsT_scale=w2_plane[:, cols],
+                    rhs=h_words[:, slots].bitcast(FP8X4),
+                    rhs_scale=h_plane[:, slots],
                     start=True,
                     stop=True,
                 )
-                copy_of[r](out=windows[r][:, tokens], in_=bank[:])
+                done = done + width
+            copy_of[r](out=z_sb[r][:, first : first + count], in_=bank[:])
+
+        windows = [keep.tile([P, T], F32, name="window%d" % r) for r in range(ROW_BLOCKS)]
+
+        def light_layer(r, half, bank_number, copy):
+            tokens = slice(half * BANK, (half + 1) * BANK)
+            bank = bank_tile([P, BANK], "y%d_%d" % (r, half), bank_number)
+            nc.tensor.matmul_mx(
+                out=bank[:],
+                lhsT=w_blocks[r].bitcast(FP4X4),
+                lhsT_scale=w_plane[:, r * P : (r + 1) * P],
+                rhs=x_sb[:, tokens].bitcast(FP8X4),
+                rhs_scale=x_plane[:, tokens],
+                start=True,
+                stop=True,
+            )
+            copy(out=windows[r][:, tokens], in_=bank[:])
 
         def scatter(r, first, count):
             target = windows[r][:].indirect(listed(first, count))
@@ -194,42 +217,58 @@ def tile_moe_cas_glu_silu_kernel(
             nc.tensor.matmul_mx(
                 out=bank_tile([P, BANK], "warm_pe%d" % half, 2 + half)[:],
                 lhsT=w1_sb[:, 0:P].bitcast(FP8X4),
-                lhsT_scale=x_plane[:, 0:P],
+                lhsT_scale=w1_plane[:, 0:P],
                 rhs=w1_sb[:].bitcast(FP8X4),
-                rhs_scale=x_plane[:, half * BANK : (half + 1) * BANK],
+                rhs_scale=w1_plane,
                 start=True,
                 stop=True,
             )
-        nc.vector.tensor_copy(slot_plane[:], x_plane.indirect(offsets[:]))
-        for c in range(CHUNKS):
-            gather_words(c)
-        gate_half(0)
-        for c in range(CHUNKS):
-            if c + 1 < CHUNKS:
-                gate_half(c + 1)
-            product_half(c)
         half = S // 2
 
-        def store(r):
-            nc.sync.dma_start(out=out[r * P : (r + 1) * P, :], in_=windows[r][:])
+        def store(r, queue):
+            queue.dma_start(out=out[r * P : (r + 1) * P, :], in_=windows[r][:])
 
-        quantise_hidden(0, 1, 4)
-        quantise_hidden(1, 1, 5)
-        quantise_hidden(2, 2, 7)
-        light_layer(0, (0, 1))
-        light_layer(1, (2, 3))
-        for piece in range(2):
-            for r in range(2):
-                second_layer(r, piece * half, half, 4 + r + 2 * piece)
-                scatter(r, piece * half, half)
-        store(0)
-        store(1)
-        light_layer(2, (0, 1))
-        light_layer(3, (2, 3))
-        second_layer(2, 0, S, 4)
-        second_layer(3, 0, S, 5)
+        by_vector, by_scalar = nc.vector.tensor_copy, nc.scalar.copy
+        nc.vector.tensor_copy(slot_plane[:], x_plane.indirect(offsets[:]))
+        w1_dealt = deal_words("w1_dealt", w1_sb)
+        w3_dealt = deal_words("w3_dealt", w3_sb)
+        w1_dealt_plane = deal_scales("w1_dealt_plane", w1_plane)
+        gather_words(0, 1, "slots0")
+        gather_words(1, 1, "slots1")
+        w3_dealt_plane = deal_scales("w3_dealt_plane", w3_plane)
+        gather_words(2, 2, "w3_sb")
+        gate_half(0, 0)
+        gate_half(1, 1)
+        product_half(0, 4)
+        product_half(1, 5)
+        gate_half(2, 2)
+        gate_half(3, 3)
+        product_half(2, 6)
+        product_half(3, 7)
+        quantise_hidden(0, 2)
+        quantise_hidden(2, 2)
+        light_layer(1, 0, 0, by_scalar)
+        light_layer(1, 1, 1, by_scalar)
+        light_layer(0, 0, 4, by_vector)
+        light_layer(0, 1, 5, by_vector)
+        second_layer(1, 0, (half,), 2)
+        second_layer(0, 0, (half,), 3)
+        scatter(1, 0, half)
+        scatter(0, 0, half)
+        light_layer(2, 1, 0, by_scalar)
+        light_layer(3, 0, 1, by_scalar)
+        light_layer(2, 0, 6, by_scalar)
+        light_layer(3, 1, 7, by_scalar)
+        second_layer(0, half, (half,), 4)
+        second_layer(3, 0, (S,), 2)
+        second_layer(2, 0, (S,), 5)
+        second_layer(1, half, (half,), 0)
+        scatter(0, half, half)
+        store(0, nc.sync)
         scatter(2, 0, S)
-        store(2)
-        scatter(3, 0, half)
-        scatter(3, half, half)
-        store(3)
+        store(2, nc.sync)
+        scatter(3, 0, P)
+        scatter(1, half, half)
+        scatter(3, P, S - P)
+        store(1, nc.scalar)
+        store(3, nc.scalar)

@@ -80,17 +80,17 @@ def tile_moe_cas_glu_silu_kernel(
         w_sb = keep.tile([P, 2 * N], U8, name="w_sb", align_bytes=64)
 
         nc.sync.dma_start(offsets[:], offs)
-        load_repeated(x_plane, x_scales, (0, 1), nc.scalar)
-        load_repeated(x_plane, x_scales, (2, 3), nc.sync)
-        w1_sb = load_words("w1_sb", w1_words, nc.scalar)
-        x_sb = load_words("x_sb", x_words, nc.sync)
-        load_upper_full(w1_plane, w1_scales, nc.scalar)
+        load_repeated(x_plane, x_scales, (0, 1, 2), nc.scalar)
+        load_repeated(x_plane, x_scales, (3,), nc.sync)
+        w1_sb = load_words("w1_sb", w1_words, nc.sync)
+        x_sb = load_words("x_sb", x_words, nc.scalar)
+        load_upper_full(w1_plane, w1_scales, nc.sync)
         load_lower(w_plane, w_scales, nc.gpsimd)
-        load_lower_full(w1_plane, w1_scales, nc.scalar)
-        load_upper_full(w3_plane, w3_scales, nc.scalar)
+        load_lower_full(w1_plane, w1_scales, nc.sync)
+        load_lower_full(w3_plane, w3_scales, nc.scalar)
         nc.scalar.activation(out=warm[:, 1:2], in_=warm[:, 0:1], func=ACT.Silu)
-        load_lower_full(w3_plane, w3_scales, nc.sync)
         w3_sb = load_words("w3_sb", w3_words, nc.sync)
+        load_upper_full(w3_plane, w3_scales, nc.sync)
         nc.sync.dma_start(out=w_sb[:].bitcast(I32), in_=w_words[0].bitcast(I32))
         load_upper(w_plane, w_scales, nc.sync)
         load_upper(w2_plane, w2_scales, nc.sync)
@@ -158,7 +158,6 @@ def tile_moe_cas_glu_silu_kernel(
                 MULT,
             )
 
-        copy_of = (nc.vector.tensor_copy, nc.scalar.copy) * 2
         z_sb = [keep.tile([P, S], F32, name="z_sb%d" % r) for r in range(ROW_BLOCKS)]
         h_words = keep.tile([P, S], U32, name="h_words", align_bytes=64)
         h_plane = keep.tile([P, S], U8, name="h_plane", align_bytes=64)
@@ -171,7 +170,7 @@ def tile_moe_cas_glu_silu_kernel(
                 in_=hidden[:, first_chunk * H : (first_chunk + chunks) * H],
             )
 
-        def second_layer(r, first, widths, bank_number):
+        def second_layer(r, first, widths, bank_number, copy):
             count = sum(widths)
             cols = slice(r * P, (r + 1) * P)
             bank = bank_tile([P, count], "z%d_%d" % (r, first), bank_number)
@@ -188,7 +187,7 @@ def tile_moe_cas_glu_silu_kernel(
                     stop=True,
                 )
                 done = done + width
-            copy_of[r](out=z_sb[r][:, first : first + count], in_=bank[:])
+            copy(out=z_sb[r][:, first : first + count], in_=bank[:])
 
         windows = [keep.tile([P, T], F32, name="window%d" % r) for r in range(ROW_BLOCKS)]
 
@@ -251,18 +250,18 @@ def tile_moe_cas_glu_silu_kernel(
         light_layer(1, 1, 1, by_scalar)
         light_layer(0, 0, 4, by_vector)
         light_layer(0, 1, 5, by_vector)
-        second_layer(1, 0, (half,), 2)
-        second_layer(0, 0, (half,), 3)
+        second_layer(1, 0, (half,), 2, by_scalar)
+        second_layer(0, 0, (half,), 3, by_vector)
         scatter(1, 0, half)
         scatter(0, 0, half)
         light_layer(2, 1, 0, by_scalar)
         light_layer(3, 0, 1, by_scalar)
         light_layer(2, 0, 6, by_scalar)
         light_layer(3, 1, 7, by_scalar)
-        second_layer(0, half, (half,), 4)
-        second_layer(3, 0, (S,), 2)
-        second_layer(2, 0, (S,), 5)
-        second_layer(1, half, (half,), 0)
+        second_layer(0, half, (half,), 4, by_vector)
+        second_layer(3, 0, (S,), 2, by_scalar)
+        second_layer(2, 0, (S,), 5, by_vector)
+        second_layer(1, half, (half,), 0, by_scalar)
         scatter(0, half, half)
         store(0, nc.sync)
         scatter(2, 0, S)

@@ -14,92 +14,99 @@ U8 = mybir.dt.uint8
 FP8X4 = mybir.dt.float8_e4m3fn_x4
 FP4X4 = mybir.dt.float4_e2m1fn_x4
 ACT = mybir.ActivationFunctionType
-MULT = mybir.AluOpType.mult
 
 P = 128
+PACK = 4
+QUADRANT = 32
 BANK = 512
-CHUNKS = S // P
-ROW_BLOCKS = N // P
+LINE = 16
+WINDOWS = N // P
 LIST_ROWS = 16
+SCALE_ROWS = K // 32
+PERIOD = 14
+FIRST_REPEATED_ROW = SCALE_ROWS - PERIOD
+HALF = S // 2
 
 
 def tile_moe_cas_glu_silu_kernel(
     tc, x_words, x_scales, w_words, w_scales, w1_words, w1_scales, w3_words, w3_scales, w2_words, w2_scales, offs, out
 ):
     nc = tc.nc
+    by_vector, by_scalar = nc.vector.tensor_copy, nc.scalar.copy
     with ExitStack() as ctx:
         keep = ctx.enter_context(tc.tile_pool(name="keep", bufs=1))
         psum = ctx.enter_context(tc.psum_pool(name="psum", bufs=1))
 
-        def zeroed_plane(engine, name, width):
-            plane = keep.tile([P, width], U8, name=name, align_bytes=64)
-            engine.memset(plane[:].bitcast(I32), 0)
-            return plane
+        def bank_tile(width, name, bank):
+            return psum.tile([P, width], F32, name=name, offset=bank * 4 * BANK)
+
+        def new_plane(name, width):
+            return keep.tile([P, width], U8, name=name, align_bytes=64)[:]
 
         def load_words(name, words, queue):
             tile = keep.tile([P, words.shape[2]], I32, name=name, tag=name, align_bytes=64)
             queue.dma_start(out=tile[:], in_=words[0].rearrange("p n d -> p (n d)").bitcast(I32))
             return tile
 
-        def bank_tile(shape, name, bank):
-            return psum.tile(shape, F32, name=name, offset=bank * 4 * BANK)
+        def load_upper_rows(plane, scales, first_partition, periods, queue):
+            rows = scales[0].bitcast(I32)[FIRST_REPEATED_ROW:SCALE_ROWS, :]
+            source = rows.unsqueeze(0).to_broadcast([periods, PERIOD, rows.shape[1]])
+            covered = slice(first_partition, first_partition + periods * PERIOD)
+            queue.dma_start(out=plane[covered, :].bitcast(I32), in_=source)
 
-        def bare_plane(name, width):
-            return keep.tile([P, width], U8, name=name, align_bytes=64)[:]
+        def load_lower_rows(plane, scales, rows, queue):
+            queue.dma_start(out=plane[0:rows, :].bitcast(I32), in_=scales[0].bitcast(I32)[0:rows, :])
 
-        def load_upper(plane, scales, queue):
-            rows = scales[0].bitcast(I32)[2:16, :]
-            source = rows.unsqueeze(0).to_broadcast([5, 14, rows.shape[1]])
-            queue.dma_start(out=plane[30:100, :].bitcast(I32), in_=source)
+        def load_token_rows(plane, quadrants, queue):
+            by_quadrant = x_scales[0].bitcast(I32).rearrange("(q r) n -> q r n", r=PACK)
+            for q in quadrants:
+                source = by_quadrant[q].unsqueeze(0).to_broadcast([QUADRANT // PACK, PACK, by_quadrant.shape[2]])
+                queue.dma_start(out=plane[QUADRANT * q : QUADRANT * (q + 1), :].bitcast(I32), in_=source)
 
-        def load_lower(plane, scales, queue):
-            queue.dma_start(out=plane[0:4, :].bitcast(I32), in_=scales[0].bitcast(I32)[0:4, :])
+        read_by_matmul = (30, 5)
+        read_by_copy = (16, 8)
 
-        def load_upper_full(plane, scales, queue):
-            rows = scales[0].bitcast(I32)[2:16, :]
-            source = rows.unsqueeze(0).to_broadcast([8, 14, rows.shape[1]])
-            queue.dma_start(out=plane[16:128, :].bitcast(I32), in_=source)
-
-        def load_lower_full(plane, scales, queue):
-            queue.dma_start(out=plane[0:16, :].bitcast(I32), in_=scales[0].bitcast(I32))
-
-        def load_repeated(plane, scales, rows, queue):
-            by_quadrant = scales[0].bitcast(I32).rearrange("(q r) n -> q r n", r=4)
-            for q in rows:
-                source = by_quadrant[q].unsqueeze(0).to_broadcast([8, 4, by_quadrant.shape[2]])
-                queue.dma_start(out=plane[32 * q : 32 * (q + 1), :].bitcast(I32), in_=source)
-
-        x_plane = bare_plane("x_plane", T)
-        warm = keep.tile([P, 2], F32, name="warm")
-        nc.vector.memset(warm[:, 0:1], 0.0)
-        w1_plane = bare_plane("w1_plane", H)
-        w3_plane = bare_plane("w3_plane", H)
-        w_plane = bare_plane("w_plane", N)
-        w2_plane = bare_plane("w2_plane", N)
+        x_plane = new_plane("x_plane", T)
+        table_probe = keep.tile([P, 2], F32, name="table_probe")
+        nc.vector.memset(table_probe[:, 0:1], 0.0)
+        w1_plane = new_plane("w1_plane", H)
+        w3_plane = new_plane("w3_plane", H)
+        w_plane = new_plane("w_plane", N)
+        w2_plane = new_plane("w2_plane", N)
         offsets = keep.tile([P, S // LIST_ROWS], U16, name="offsets")
         w_sb = keep.tile([P, 2 * N], U8, name="w_sb", align_bytes=64)
 
         nc.sync.dma_start(offsets[:], offs)
-        load_repeated(x_plane, x_scales, (0, 1, 2), nc.scalar)
-        load_repeated(x_plane, x_scales, (3,), nc.sync)
+        load_token_rows(x_plane, (0, 1, 2), nc.scalar)
+        load_token_rows(x_plane, (3,), nc.sync)
         w1_sb = load_words("w1_sb", w1_words, nc.sync)
         x_sb = load_words("x_sb", x_words, nc.scalar)
-        load_upper_full(w1_plane, w1_scales, nc.sync)
-        load_lower(w_plane, w_scales, nc.gpsimd)
-        load_lower_full(w1_plane, w1_scales, nc.sync)
-        load_lower_full(w3_plane, w3_scales, nc.scalar)
-        nc.scalar.activation(out=warm[:, 1:2], in_=warm[:, 0:1], func=ACT.Silu)
+        load_upper_rows(w1_plane, w1_scales, *read_by_copy, nc.sync)
+        load_lower_rows(w_plane, w_scales, PACK, nc.gpsimd)
+        load_lower_rows(w1_plane, w1_scales, SCALE_ROWS, nc.sync)
+        load_lower_rows(w3_plane, w3_scales, SCALE_ROWS, nc.scalar)
+        nc.scalar.activation(out=table_probe[:, 1:2], in_=table_probe[:, 0:1], func=ACT.Silu)
         w3_sb = load_words("w3_sb", w3_words, nc.sync)
-        load_upper_full(w3_plane, w3_scales, nc.sync)
+        load_upper_rows(w3_plane, w3_scales, *read_by_copy, nc.sync)
         nc.sync.dma_start(out=w_sb[:].bitcast(I32), in_=w_words[0].bitcast(I32))
-        load_upper(w_plane, w_scales, nc.sync)
-        load_upper(w2_plane, w2_scales, nc.sync)
+        load_upper_rows(w_plane, w_scales, *read_by_matmul, nc.sync)
+        load_upper_rows(w2_plane, w2_scales, *read_by_matmul, nc.sync)
         w2_sb = load_words("w2_sb", w2_words, nc.sync)
-        load_lower(w2_plane, w2_scales, nc.sync)
-        w_blocks = [w_sb[:, 2 * r * P : 2 * (r + 1) * P] for r in range(ROW_BLOCKS)]
+        load_lower_rows(w2_plane, w2_scales, PACK, nc.sync)
 
         def listed(first, count):
             return offsets[:, first // LIST_ROWS : (first + count) // LIST_ROWS]
+
+        def mx_pass(target, stationary, stationary_plane, moving, moving_plane):
+            nc.tensor.matmul_mx(
+                out=target,
+                lhsT=stationary,
+                lhsT_scale=stationary_plane,
+                rhs=moving,
+                rhs_scale=moving_plane,
+                start=True,
+                stop=True,
+            )
 
         slot_plane = keep.tile([P, S], U8, name="slot_plane", align_bytes=64)
         slot_words = {}
@@ -110,98 +117,81 @@ def tile_moe_cas_glu_silu_kernel(
             for c in range(chunks):
                 slot_words[first_chunk + c] = tile[:, c * P : (c + 1) * P]
 
-        def deal_words(name, words):
-            dealt = keep.tile([P, H], U32, name=name, align_bytes=64)
-            nc.scalar.copy(
-                out=dealt[:].rearrange("p (t g m) -> p g t m", t=4, m=4),
-                in_=words[:].bitcast(U32).rearrange("p (g m t) -> p g t m", m=4, t=4),
+        def deal(name, source, dtype, per_line, copy):
+            dealt = keep.tile([P, H], dtype, name=name, align_bytes=64)
+            copy(
+                out=dealt[:].rearrange("p (t g m) -> p g t m", t=PACK, m=per_line),
+                in_=source.rearrange("p (g m t) -> p g t m", m=per_line, t=PACK),
             )
             return dealt
 
-        def deal_scales(name, plane):
-            dealt = keep.tile([P, H], U8, name=name, align_bytes=64)
-            nc.vector.tensor_copy(
-                dealt[:].rearrange("p (t g m) -> p g t m", t=4, m=16),
-                plane.rearrange("p (g m t) -> p g t m", m=16, t=4),
-            )
-            return dealt
-
-        def first_pass(c, bank_number, words, plane):
-            bank = bank_tile([P, BANK], "a%d_%d" % (c, bank_number), bank_number)
-            for t in range(4):
-                cols = slice(t * P, (t + 1) * P)
-                nc.tensor.matmul_mx(
-                    out=bank[:, cols],
-                    lhsT=words[:, cols].bitcast(FP8X4),
-                    lhsT_scale=plane[:, cols],
-                    rhs=slot_words[c].bitcast(FP8X4),
-                    rhs_scale=slot_plane[:, c * P : (c + 1) * P],
-                    start=True,
-                    stop=True,
+        def first_layer_sums(c, bank_number, words, plane):
+            bank = bank_tile(BANK, "a%d_%d" % (c, bank_number), bank_number)
+            for t in range(PACK):
+                block = slice(t * P, (t + 1) * P)
+                mx_pass(
+                    bank[:, block],
+                    words[:, block].bitcast(FP8X4),
+                    plane[:, block],
+                    slot_words[c].bitcast(FP8X4),
+                    slot_plane[:, c * P : (c + 1) * P],
                 )
-            return bank[:].rearrange("p (t j) -> p j t", t=4)
+            return bank[:].rearrange("p (t j) -> p j t", t=PACK)
 
+        slot_by_slot = "p (j t) -> p j t"
         gates = {}
-        hidden = keep.tile([P, 4 * S], BF16, name="hidden", align_bytes=64)
+        hidden = keep.tile([P, PACK * S], BF16, name="hidden", align_bytes=64)
 
-        def gate_half(c, bank_number):
-            sums = first_pass(c, bank_number, w1_dealt, w1_dealt_plane)
+        def gate(c, bank_number):
+            sums = first_layer_sums(c, bank_number, w1_dealt, w1_dealt_plane)
             gates[c] = keep.tile([P, H], F32, name="gate%d" % c)
-            nc.scalar.activation(out=gates[c][:].rearrange("p (j t) -> p j t", t=4), in_=sums, func=ACT.Silu)
+            nc.scalar.activation(out=gates[c][:].rearrange(slot_by_slot, t=PACK), in_=sums, func=ACT.Silu)
 
-        def product_half(c, bank_number):
-            sums = first_pass(c, bank_number, w3_dealt, w3_dealt_plane)
+        def product(c, bank_number):
+            sums = first_layer_sums(c, bank_number, w3_dealt, w3_dealt_plane)
             nc.vector.tensor_tensor(
-                hidden[:, c * H : (c + 1) * H].rearrange("p (j t) -> p j t", t=4),
+                hidden[:, c * H : (c + 1) * H].rearrange(slot_by_slot, t=PACK),
                 sums,
-                gates[c][:].rearrange("p (j t) -> p j t", t=4),
-                MULT,
+                gates[c][:].rearrange(slot_by_slot, t=PACK),
+                mybir.AluOpType.mult,
             )
 
-        z_sb = [keep.tile([P, S], F32, name="z_sb%d" % r) for r in range(ROW_BLOCKS)]
+        z_sb = [keep.tile([P, S], F32, name="z_sb%d" % r) for r in range(WINDOWS)]
         h_words = keep.tile([P, S], U32, name="h_words", align_bytes=64)
         h_plane = keep.tile([P, S], U8, name="h_plane", align_bytes=64)
 
-        def quantise_hidden(first_chunk, chunks):
-            slots = slice(first_chunk * P, (first_chunk + chunks) * P)
+        def quantise_hidden(first, count):
+            slots = slice(first, first + count)
             nc.vector.quantize_mx(
                 out=h_words[:, slots].bitcast(FP8X4),
                 scales=h_plane[:, slots],
-                in_=hidden[:, first_chunk * H : (first_chunk + chunks) * H],
+                in_=hidden[:, PACK * first : PACK * (first + count)],
             )
 
-        def second_layer(r, first, widths, bank_number, copy):
-            count = sum(widths)
-            cols = slice(r * P, (r + 1) * P)
-            bank = bank_tile([P, count], "z%d_%d" % (r, first), bank_number)
-            done = 0
-            for width in widths:
-                slots = slice(first + done, first + done + width)
-                nc.tensor.matmul_mx(
-                    out=bank[:, done : done + width],
-                    lhsT=w2_sb[:, cols].bitcast(FP8X4),
-                    lhsT_scale=w2_plane[:, cols],
-                    rhs=h_words[:, slots].bitcast(FP8X4),
-                    rhs_scale=h_plane[:, slots],
-                    start=True,
-                    stop=True,
-                )
-                done = done + width
-            copy(out=z_sb[r][:, first : first + count], in_=bank[:])
+        def second_layer(r, first, count, bank_number, copy):
+            rows = slice(r * P, (r + 1) * P)
+            slots = slice(first, first + count)
+            bank = bank_tile(count, "z%d_%d" % (r, first), bank_number)
+            mx_pass(
+                bank[:],
+                w2_sb[:, rows].bitcast(FP8X4),
+                w2_plane[:, rows],
+                h_words[:, slots].bitcast(FP8X4),
+                h_plane[:, slots],
+            )
+            copy(out=z_sb[r][:, slots], in_=bank[:])
 
-        windows = [keep.tile([P, T], F32, name="window%d" % r) for r in range(ROW_BLOCKS)]
+        windows = [keep.tile([P, T], F32, name="window%d" % r) for r in range(WINDOWS)]
 
-        def light_layer(r, half, bank_number, copy):
-            tokens = slice(half * BANK, (half + 1) * BANK)
-            bank = bank_tile([P, BANK], "y%d_%d" % (r, half), bank_number)
-            nc.tensor.matmul_mx(
-                out=bank[:],
-                lhsT=w_blocks[r].bitcast(FP4X4),
-                lhsT_scale=w_plane[:, r * P : (r + 1) * P],
-                rhs=x_sb[:, tokens].bitcast(FP8X4),
-                rhs_scale=x_plane[:, tokens],
-                start=True,
-                stop=True,
+        def light_layer(r, part, bank_number, copy):
+            tokens = slice(part * BANK, (part + 1) * BANK)
+            bank = bank_tile(BANK, "y%d_%d" % (r, part), bank_number)
+            mx_pass(
+                bank[:],
+                w_sb[:, 2 * r * P : 2 * (r + 1) * P].bitcast(FP4X4),
+                w_plane[:, r * P : (r + 1) * P],
+                x_sb[:, tokens].bitcast(FP8X4),
+                x_plane[:, tokens],
             )
             copy(out=windows[r][:, tokens], in_=bank[:])
 
@@ -212,62 +202,60 @@ def tile_moe_cas_glu_silu_kernel(
             else:
                 nc.scalar.activation(target, z_sb[r][:, first : first + count], ACT.Copy)
 
-        for half in range(2):
-            nc.tensor.matmul_mx(
-                out=bank_tile([P, BANK], "warm_pe%d" % half, 2 + half)[:],
-                lhsT=w1_sb[:, 0:P].bitcast(FP8X4),
-                lhsT_scale=w1_plane[:, 0:P],
-                rhs=w1_sb[:].bitcast(FP8X4),
-                rhs_scale=w1_plane,
-                start=True,
-                stop=True,
+        def store(r):
+            nc.sync.dma_start(out=out[r * P : (r + 1) * P, :], in_=windows[r][:])
+
+        for bank_number in (2, 3):
+            mx_pass(
+                bank_tile(BANK, "warm_up%d" % bank_number, bank_number)[:],
+                w1_sb[:, 0:P].bitcast(FP8X4),
+                w1_plane[:, 0:P],
+                w1_sb[:].bitcast(FP8X4),
+                w1_plane,
             )
-        half = S // 2
 
-        def store(r, queue):
-            queue.dma_start(out=out[r * P : (r + 1) * P, :], in_=windows[r][:])
-
-        by_vector, by_scalar = nc.vector.tensor_copy, nc.scalar.copy
         nc.vector.tensor_copy(slot_plane[:], x_plane.indirect(offsets[:]))
-        w1_dealt = deal_words("w1_dealt", w1_sb)
-        w3_dealt = deal_words("w3_dealt", w3_sb)
-        w1_dealt_plane = deal_scales("w1_dealt_plane", w1_plane)
+        w1_dealt = deal("w1_dealt", w1_sb[:].bitcast(U32), U32, LINE // 4, by_scalar)
+        w3_dealt = deal("w3_dealt", w3_sb[:].bitcast(U32), U32, LINE // 4, by_scalar)
+        w1_dealt_plane = deal("w1_dealt_plane", w1_plane, U8, LINE, by_vector)
         gather_words(0, 1, "slots0")
         gather_words(1, 1, "slots1")
-        w3_dealt_plane = deal_scales("w3_dealt_plane", w3_plane)
+        w3_dealt_plane = deal("w3_dealt_plane", w3_plane, U8, LINE, by_vector)
         gather_words(2, 2, "w3_sb")
-        gate_half(0, 0)
-        gate_half(1, 1)
-        product_half(0, 4)
-        product_half(1, 5)
-        gate_half(2, 2)
-        gate_half(3, 3)
-        product_half(2, 6)
-        product_half(3, 7)
-        quantise_hidden(0, 2)
-        quantise_hidden(2, 2)
+
+        for pair in ((0, 1), (2, 3)):
+            for c in pair:
+                gate(c, c)
+            for c in pair:
+                product(c, 4 + c)
+        quantise_hidden(0, HALF)
+        quantise_hidden(HALF, HALF)
+
         light_layer(1, 0, 0, by_scalar)
         light_layer(1, 1, 1, by_scalar)
         light_layer(0, 0, 4, by_vector)
         light_layer(0, 1, 5, by_vector)
-        second_layer(1, 0, (half,), 2, by_scalar)
-        second_layer(0, 0, (half,), 3, by_vector)
-        scatter(1, 0, half)
-        scatter(0, 0, half)
+        second_layer(1, 0, HALF, 2, by_scalar)
+        second_layer(0, 0, HALF, 3, by_vector)
+        scatter(1, 0, HALF)
+        scatter(0, 0, HALF)
+
         light_layer(2, 1, 0, by_scalar)
-        light_layer(3, 0, 1, by_scalar)
         light_layer(2, 0, 6, by_scalar)
+        light_layer(3, 0, 1, by_scalar)
         light_layer(3, 1, 7, by_scalar)
-        second_layer(0, half, (half,), 4, by_vector)
-        second_layer(3, 0, (S,), 2, by_scalar)
-        second_layer(2, 0, (S,), 5, by_vector)
-        second_layer(1, half, (half,), 0, by_scalar)
-        scatter(0, half, half)
-        store(0, nc.sync)
-        scatter(2, 0, S)
-        store(2, nc.sync)
+        second_layer(0, HALF, HALF, 4, by_vector)
+        second_layer(3, 0, S, 2, by_scalar)
+        second_layer(2, 0, HALF, 5, by_vector)
+        second_layer(1, HALF, HALF, 0, by_scalar)
+        second_layer(2, HALF, HALF, 3, by_scalar)
+
+        scatter(0, HALF, HALF)
+        store(0)
         scatter(3, 0, P)
-        scatter(1, half, half)
+        scatter(1, HALF, HALF)
+        store(1)
+        scatter(2, 0, S)
+        store(2)
         scatter(3, P, S - P)
-        store(1, nc.scalar)
-        store(3, nc.scalar)
+        store(3)

@@ -77,21 +77,21 @@ def tile_moe_cas_glu_silu_kernel(
         w_sb = keep.tile([P, 2 * N], U8, name="w_sb", align_bytes=64)
 
         nc.sync.dma_start(offsets[:], offs)
-        load_token_rows(x_plane, (0, 1, 2), nc.scalar)
-        load_token_rows(x_plane, (3,), nc.sync)
-        w1_sb = load_words("w1_sb", w1_words, nc.sync)
+        load_token_rows(x_plane, (0, 1), nc.scalar)
+        load_token_rows(x_plane, (2, 3), nc.sync)
         x_sb = load_words("x_sb", x_words, nc.scalar)
-        load_upper_rows(w1_plane, w1_scales, *read_by_copy, nc.sync)
-        load_lower_rows(w_plane, w_scales, PACK, nc.gpsimd)
-        load_lower_rows(w1_plane, w1_scales, SCALE_ROWS, nc.sync)
-        load_lower_rows(w3_plane, w3_scales, SCALE_ROWS, nc.scalar)
-        nc.scalar.activation(out=table_probe[:, 1:2], in_=table_probe[:, 0:1], func=ACT.Silu)
-        w3_sb = load_words("w3_sb", w3_words, nc.sync)
-        load_upper_rows(w3_plane, w3_scales, *read_by_copy, nc.sync)
         nc.sync.dma_start(out=w_sb[:].bitcast(I32), in_=w_words[0].bitcast(I32))
         load_upper_rows(w_plane, w_scales, *read_by_matmul, nc.sync)
-        load_upper_rows(w2_plane, w2_scales, *read_by_matmul, nc.sync)
+        load_lower_rows(w_plane, w_scales, PACK, nc.gpsimd)
+        load_upper_rows(w1_plane, w1_scales, *read_by_copy, nc.scalar)
+        load_lower_rows(w1_plane, w1_scales, SCALE_ROWS, nc.scalar)
+        nc.scalar.activation(out=table_probe[:, 1:2], in_=table_probe[:, 0:1], func=ACT.Silu)
+        w1_sb = load_words("w1_sb", w1_words, nc.sync)
+        load_upper_rows(w3_plane, w3_scales, *read_by_copy, nc.sync)
+        load_lower_rows(w3_plane, w3_scales, SCALE_ROWS, nc.sync)
+        w3_sb = load_words("w3_sb", w3_words, nc.sync)
         w2_sb = load_words("w2_sb", w2_words, nc.sync)
+        load_upper_rows(w2_plane, w2_scales, *read_by_matmul, nc.sync)
         load_lower_rows(w2_plane, w2_scales, PACK, nc.sync)
 
         def listed(first, count):
@@ -117,8 +117,8 @@ def tile_moe_cas_glu_silu_kernel(
             for c in range(chunks):
                 slot_words[first_chunk + c] = tile[:, c * P : (c + 1) * P]
 
-        def deal(name, source, dtype, per_line, copy):
-            dealt = keep.tile([P, H], dtype, name=name, align_bytes=64)
+        def deal(name, source, dtype, per_line, copy, tag=None):
+            dealt = keep.tile([P, H], dtype, name=name, tag=tag or name, align_bytes=64)
             copy(
                 out=dealt[:].rearrange("p (t g m) -> p g t m", t=PACK, m=per_line),
                 in_=source.rearrange("p (g m t) -> p g t m", m=per_line, t=PACK),
@@ -181,7 +181,10 @@ def tile_moe_cas_glu_silu_kernel(
             )
             copy(out=z_sb[r][:, slots], in_=bank[:])
 
-        windows = [keep.tile([P, T], F32, name="window%d" % r) for r in range(WINDOWS)]
+        windows = [
+            keep.tile([P, T], F32, name="window%d" % r, tag="w3_sb" if r == 2 else "window%d" % r, align_bytes=64)
+            for r in range(WINDOWS)
+        ]
 
         def light_layer(r, part, bank_number, copy):
             tokens = slice(part * BANK, (part + 1) * BANK)
@@ -205,50 +208,39 @@ def tile_moe_cas_glu_silu_kernel(
         def store(r):
             nc.sync.dma_start(out=out[r * P : (r + 1) * P, :], in_=windows[r][:])
 
-        for bank_number in (2, 3):
-            mx_pass(
-                bank_tile(BANK, "warm_up%d" % bank_number, bank_number)[:],
-                w1_sb[:, 0:P].bitcast(FP8X4),
-                w1_plane[:, 0:P],
-                w1_sb[:].bitcast(FP8X4),
-                w1_plane,
-            )
-
         nc.vector.tensor_copy(slot_plane[:], x_plane.indirect(offsets[:]))
-        w1_dealt = deal("w1_dealt", w1_sb[:].bitcast(U32), U32, LINE // 4, by_scalar)
-        w3_dealt = deal("w3_dealt", w3_sb[:].bitcast(U32), U32, LINE // 4, by_scalar)
+        gather_words(0, 4, "slots")
+        w1_dealt = deal("w1_dealt", w1_sb[:].bitcast(I32), I32, LINE // 4, by_vector)
         w1_dealt_plane = deal("w1_dealt_plane", w1_plane, U8, LINE, by_vector)
-        gather_words(0, 1, "slots0")
-        gather_words(1, 1, "slots1")
         w3_dealt_plane = deal("w3_dealt_plane", w3_plane, U8, LINE, by_vector)
-        gather_words(2, 2, "w3_sb")
+        w3_dealt = deal("w3_dealt", w3_sb[:].bitcast(I32), I32, LINE // 4, by_vector, "w3_plane")
 
-        for pair in ((0, 1), (2, 3)):
-            for c in pair:
-                gate(c, c)
-            for c in pair:
-                product(c, 4 + c)
+        light_layer(1, 0, 4, by_scalar)
+        light_layer(1, 1, 5, by_scalar)
+        light_layer(0, 0, 6, by_scalar)
+        light_layer(2, 0, 3, by_vector)
+        gate(0, 0)
+        light_layer(2, 1, 5, by_vector)
+
+        for c in range(1, 4):
+            gate(c, c)
+        product(0, 4)
+        product(1, 7)
+        product(2, 6)
         quantise_hidden(0, HALF)
+        product(3, 5)
+        second_layer(0, 0, HALF, 4, by_vector)
         quantise_hidden(HALF, HALF)
-
-        light_layer(1, 0, 0, by_scalar)
-        light_layer(1, 1, 1, by_scalar)
-        light_layer(0, 0, 4, by_vector)
-        light_layer(0, 1, 5, by_vector)
-        second_layer(1, 0, HALF, 2, by_scalar)
-        second_layer(0, 0, HALF, 3, by_vector)
-        scatter(1, 0, HALF)
-        scatter(0, 0, HALF)
-
-        light_layer(2, 1, 0, by_scalar)
-        light_layer(2, 0, 6, by_scalar)
-        light_layer(3, 0, 1, by_scalar)
+        light_layer(0, 1, 2, by_scalar)
+        light_layer(3, 0, 3, by_scalar)
         light_layer(3, 1, 7, by_scalar)
-        second_layer(0, HALF, HALF, 4, by_vector)
-        second_layer(3, 0, S, 2, by_scalar)
-        second_layer(2, 0, HALF, 5, by_vector)
-        second_layer(1, HALF, HALF, 0, by_scalar)
-        second_layer(2, HALF, HALF, 3, by_scalar)
+        second_layer(1, 0, HALF, 0, by_scalar)
+        scatter(0, 0, HALF)
+        scatter(1, 0, HALF)
+        second_layer(0, HALF, HALF, 1, by_vector)
+        second_layer(3, 0, S, 6, by_scalar)
+        second_layer(1, HALF, HALF, 5, by_scalar)
+        second_layer(2, 0, S, 2, by_scalar)
 
         scatter(0, HALF, HALF)
         store(0)

from contextlib import ExitStack

import concourse.mybir as mybir

K, T, S, H, N = 512, 1024, 512, 512, 512
FLOPS = 2 * K * N * T + 2 * S * (2 * K * H + H * N)

F32 = mybir.dt.float32
BF16 = mybir.dt.bfloat16
I32 = mybir.dt.int32
U32 = mybir.dt.uint32
U16 = mybir.dt.uint16
U8 = mybir.dt.uint8
FP8X4 = mybir.dt.float8_e4m3fn_x4
FP4X4 = mybir.dt.float4_e2m1fn_x4
ACT = mybir.ActivationFunctionType

P = 128
PACK = 4
QUADRANT = 32
BANK = 512
LINE = 16
WINDOWS = N // P
LIST_ROWS = 16
SCALE_ROWS = K // 32
PERIOD = 14
FIRST_REPEATED_ROW = SCALE_ROWS - PERIOD
HALF = S // 2


def tile_moe_cas_glu_silu_kernel(
    tc, x_words, x_scales, w_words, w_scales, w1_words, w1_scales, w3_words, w3_scales, w2_words, w2_scales, offs, out
):
    nc = tc.nc
    by_vector, by_scalar = nc.vector.tensor_copy, nc.scalar.copy
    with ExitStack() as ctx:
        keep = ctx.enter_context(tc.tile_pool(name="keep", bufs=1))
        psum = ctx.enter_context(tc.psum_pool(name="psum", bufs=1))

        def bank_tile(width, name, bank):
            return psum.tile([P, width], F32, name=name, offset=bank * 4 * BANK)

        def new_plane(name, width):
            return keep.tile([P, width], U8, name=name, align_bytes=64)[:]

        def load_words(name, words, queue):
            tile = keep.tile([P, words.shape[2]], I32, name=name, tag=name, align_bytes=64)
            queue.dma_start(out=tile[:], in_=words[0].rearrange("p n d -> p (n d)").bitcast(I32))
            return tile

        def load_upper_rows(plane, scales, first_partition, periods, queue):
            rows = scales[0].bitcast(I32)[FIRST_REPEATED_ROW:SCALE_ROWS, :]
            source = rows.unsqueeze(0).to_broadcast([periods, PERIOD, rows.shape[1]])
            covered = slice(first_partition, first_partition + periods * PERIOD)
            queue.dma_start(out=plane[covered, :].bitcast(I32), in_=source)

        def load_lower_rows(plane, scales, rows, queue):
            queue.dma_start(out=plane[0:rows, :].bitcast(I32), in_=scales[0].bitcast(I32)[0:rows, :])

        def load_token_rows(plane, quadrants, queue):
            by_quadrant = x_scales[0].bitcast(I32).rearrange("(q r) n -> q r n", r=PACK)
            for q in quadrants:
                source = by_quadrant[q].unsqueeze(0).to_broadcast([QUADRANT // PACK, PACK, by_quadrant.shape[2]])
                queue.dma_start(out=plane[QUADRANT * q : QUADRANT * (q + 1), :].bitcast(I32), in_=source)

        read_by_matmul = (30, 5)
        read_by_copy = (16, 8)

        x_plane = new_plane("x_plane", T)
        table_probe = keep.tile([P, 2], F32, name="table_probe")
        nc.vector.memset(table_probe[:, 0:1], 0.0)
        w1_plane = new_plane("w1_plane", H)
        w3_plane = new_plane("w3_plane", H)
        w_plane = new_plane("w_plane", N)
        w2_plane = new_plane("w2_plane", N)
        offsets = keep.tile([P, S // LIST_ROWS], U16, name="offsets")
        w_sb = keep.tile([P, 2 * N], U8, name="w_sb", align_bytes=64)

        nc.sync.dma_start(offsets[:], offs)
        load_token_rows(x_plane, (0, 1), nc.scalar)
        load_token_rows(x_plane, (2, 3), nc.sync)
        x_sb = load_words("x_sb", x_words, nc.scalar)
        nc.sync.dma_start(out=w_sb[:].bitcast(I32), in_=w_words[0].bitcast(I32))
        load_upper_rows(w_plane, w_scales, *read_by_matmul, nc.sync)
        load_lower_rows(w_plane, w_scales, PACK, nc.gpsimd)
        load_upper_rows(w1_plane, w1_scales, *read_by_copy, nc.scalar)
        load_lower_rows(w1_plane, w1_scales, SCALE_ROWS, nc.scalar)
        nc.scalar.activation(out=table_probe[:, 1:2], in_=table_probe[:, 0:1], func=ACT.Silu)
        w1_sb = load_words("w1_sb", w1_words, nc.sync)
        load_upper_rows(w3_plane, w3_scales, *read_by_copy, nc.sync)
        load_lower_rows(w3_plane, w3_scales, SCALE_ROWS, nc.sync)
        w3_sb = load_words("w3_sb", w3_words, nc.sync)
        w2_sb = load_words("w2_sb", w2_words, nc.sync)
        load_upper_rows(w2_plane, w2_scales, *read_by_matmul, nc.sync)
        load_lower_rows(w2_plane, w2_scales, PACK, nc.sync)

        def listed(first, count):
            return offsets[:, first // LIST_ROWS : (first + count) // LIST_ROWS]

        def mx_pass(target, stationary, stationary_plane, moving, moving_plane):
            nc.tensor.matmul_mx(
                out=target,
                lhsT=stationary,
                lhsT_scale=stationary_plane,
                rhs=moving,
                rhs_scale=moving_plane,
                start=True,
                stop=True,
            )

        slot_plane = keep.tile([P, S], U8, name="slot_plane", align_bytes=64)
        slot_words = {}

        def gather_words(first_chunk, chunks, tag):
            tile = keep.tile([P, chunks * P], U32, name="slot_words%d" % first_chunk, tag=tag, align_bytes=64)
            nc.vector.tensor_copy(tile[:], x_sb[:].bitcast(U32).indirect(listed(first_chunk * P, chunks * P)))
            for c in range(chunks):
                slot_words[first_chunk + c] = tile[:, c * P : (c + 1) * P]

        def deal(name, source, dtype, per_line, copy, tag=None):
            dealt = keep.tile([P, H], dtype, name=name, tag=tag or name, align_bytes=64)
            copy(
                out=dealt[:].rearrange("p (t g m) -> p g t m", t=PACK, m=per_line),
                in_=source.rearrange("p (g m t) -> p g t m", m=per_line, t=PACK),
            )
            return dealt

        def first_layer_sums(c, bank_number, words, plane):
            bank = bank_tile(BANK, "a%d_%d" % (c, bank_number), bank_number)
            for t in range(PACK):
                block = slice(t * P, (t + 1) * P)
                mx_pass(
                    bank[:, block],
                    words[:, block].bitcast(FP8X4),
                    plane[:, block],
                    slot_words[c].bitcast(FP8X4),
                    slot_plane[:, c * P : (c + 1) * P],
                )
            return bank[:].rearrange("p (t j) -> p j t", t=PACK)

        slot_by_slot = "p (j t) -> p j t"
        gates = {}
        hidden = keep.tile([P, PACK * S], BF16, name="hidden", align_bytes=64)

        def gate(c, bank_number):
            sums = first_layer_sums(c, bank_number, w1_dealt, w1_dealt_plane)
            gates[c] = keep.tile([P, H], F32, name="gate%d" % c)
            nc.scalar.activation(out=gates[c][:].rearrange(slot_by_slot, t=PACK), in_=sums, func=ACT.Silu)

        def product(c, bank_number):
            sums = first_layer_sums(c, bank_number, w3_dealt, w3_dealt_plane)
            nc.vector.tensor_tensor(
                hidden[:, c * H : (c + 1) * H].rearrange(slot_by_slot, t=PACK),
                sums,
                gates[c][:].rearrange(slot_by_slot, t=PACK),
                mybir.AluOpType.mult,
            )

        z_sb = [keep.tile([P, S], F32, name="z_sb%d" % r) for r in range(WINDOWS)]
        h_words = keep.tile([P, S], U32, name="h_words", align_bytes=64)
        h_plane = keep.tile([P, S], U8, name="h_plane", align_bytes=64)

        def quantise_hidden(first, count):
            slots = slice(first, first + count)
            nc.vector.quantize_mx(
                out=h_words[:, slots].bitcast(FP8X4),
                scales=h_plane[:, slots],
                in_=hidden[:, PACK * first : PACK * (first + count)],
            )

        def second_layer(r, first, count, bank_number, copy):
            rows = slice(r * P, (r + 1) * P)
            slots = slice(first, first + count)
            bank = bank_tile(count, "z%d_%d" % (r, first), bank_number)
            mx_pass(
                bank[:],
                w2_sb[:, rows].bitcast(FP8X4),
                w2_plane[:, rows],
                h_words[:, slots].bitcast(FP8X4),
                h_plane[:, slots],
            )
            copy(out=z_sb[r][:, slots], in_=bank[:])

        windows = [
            keep.tile([P, T], F32, name="window%d" % r, tag="w3_sb" if r == 2 else "window%d" % r, align_bytes=64)
            for r in range(WINDOWS)
        ]

        def light_layer(r, part, bank_number, copy):
            tokens = slice(part * BANK, (part + 1) * BANK)
            bank = bank_tile(BANK, "y%d_%d" % (r, part), bank_number)
            mx_pass(
                bank[:],
                w_sb[:, 2 * r * P : 2 * (r + 1) * P].bitcast(FP4X4),
                w_plane[:, r * P : (r + 1) * P],
                x_sb[:, tokens].bitcast(FP8X4),
                x_plane[:, tokens],
            )
            copy(out=windows[r][:, tokens], in_=bank[:])

        def scatter(r, first, count):
            target = windows[r][:].indirect(listed(first, count))
            if r % 2 == 0:
                nc.vector.tensor_copy(target, z_sb[r][:, first : first + count])
            else:
                nc.scalar.activation(target, z_sb[r][:, first : first + count], ACT.Copy)

        def store(r):
            nc.sync.dma_start(out=out[r * P : (r + 1) * P, :], in_=windows[r][:])

        nc.vector.tensor_copy(slot_plane[:], x_plane.indirect(offsets[:]))
        gather_words(0, 4, "slots")
        w1_dealt = deal("w1_dealt", w1_sb[:].bitcast(I32), I32, LINE // 4, by_vector)
        w1_dealt_plane = deal("w1_dealt_plane", w1_plane, U8, LINE, by_vector)
        w3_dealt_plane = deal("w3_dealt_plane", w3_plane, U8, LINE, by_vector)
        w3_dealt = deal("w3_dealt", w3_sb[:].bitcast(I32), I32, LINE // 4, by_vector, "w3_plane")

        light_layer(1, 0, 4, by_scalar)
        light_layer(1, 1, 5, by_scalar)
        light_layer(0, 0, 6, by_scalar)
        light_layer(2, 0, 3, by_vector)
        gate(0, 0)
        light_layer(2, 1, 5, by_vector)

        for c in range(1, 4):
            gate(c, c)
        product(0, 4)
        product(1, 7)
        product(2, 6)
        quantise_hidden(0, HALF)
        product(3, 5)
        second_layer(0, 0, HALF, 4, by_vector)
        quantise_hidden(HALF, HALF)
        light_layer(0, 1, 2, by_scalar)
        light_layer(3, 0, 3, by_scalar)
        light_layer(3, 1, 7, by_scalar)
        second_layer(1, 0, HALF, 0, by_scalar)
        scatter(0, 0, HALF)
        scatter(1, 0, HALF)
        second_layer(0, HALF, HALF, 1, by_vector)
        second_layer(3, 0, S, 6, by_scalar)
        second_layer(1, HALF, HALF, 5, by_scalar)
        second_layer(2, 0, S, 2, by_scalar)

        scatter(0, HALF, HALF)
        store(0)
        scatter(3, 0, P)
        scatter(1, HALF, HALF)
        store(1)
        scatter(2, 0, S)
        store(2)
        scatter(3, P, S - P)
        store(3)
